import numpy as np
import ml_dtypes


def mxq(x, axis, fmt="e4m3"):
    dtype, down = {"e4m3": (ml_dtypes.float8_e4m3fn, 7), "e5m2": (ml_dtypes.float8_e5m2, 14)}[fmt]
    v = np.moveaxis(np.asarray(x, np.float32).astype(ml_dtypes.bfloat16).astype(np.float64), axis, -1)
    blocks = v.reshape(v.shape[:-1] + (-1, 32))
    amax = np.abs(blocks).max(-1, keepdims=True)
    byte = np.maximum(np.where(amax > 0, np.frexp(amax)[1] - 1 + 127, 0) - down, 1)
    scale = np.exp2(byte - 127.0)
    codes = (blocks / scale).astype(np.float32).astype(dtype).astype(np.float64)
    return np.moveaxis((codes * scale).reshape(v.shape), -1, axis)


WIDE = False


def mx_kscale(k):
    if not WIDE:
        return np.ones(k)
    levels = np.array([10, -10, 5, -5, 0])
    if k % 512:
        return np.exp2(np.random.permutation(np.resize(levels, k // 32))).repeat(32)
    a = np.empty((k // 512, 16))
    for p in range(k // 512):
        a[p, :8] = np.random.permutation(np.resize(levels, 8))
        for g in range(8):
            far = levels[np.abs(levels - a[p, g]) >= 10]
            a[p, g + 8] = far[np.random.randint(len(far))]
    return np.exp2(a.ravel()).repeat(32)


def f64(x):
    return np.asarray(x).astype(np.float64)


def striped(idx):
    return np.tile(idx.reshape(-1, 16).T, (8, 1)).astype(np.uint16)


def unstriped(offs):
    return offs[:16].T.reshape(-1).astype(np.int64)


E2M1 = np.array([0.0, 0.5, 1.0, 1.5, 2.0, 3.0, 4.0, 6.0, -0.0, -0.5, -1.0, -1.5, -2.0, -3.0, -4.0, -6.0])


def pack_weight(w, fmt):
    k, n = w.shape
    w = f64(np.asarray(w, np.float32).astype(ml_dtypes.bfloat16)).reshape(k // 32, 32, n)
    amax = np.abs(w).max(1)
    if fmt == "e4m3":
        byte = np.frexp(amax)[1] - 1 + 127 - 7
    else:
        mant, ex = np.frexp(amax / 6.0)
        byte = np.where(mant > 0.5, ex, ex - 1) + 127
    byte = np.clip(np.where(amax > 0, byte, 1), 1, 254)
    scaled = (w * np.exp2(127.0 - byte)[:, None, :]).reshape(k, n).astype(np.float32)
    by_word = np.ascontiguousarray(scaled.reshape(k // 512, 128, 4, n).transpose(0, 1, 3, 2))
    if fmt == "e4m3":
        words = by_word.astype(ml_dtypes.float8_e4m3fn).view(np.uint8)
    else:
        c = by_word.astype(ml_dtypes.float4_e2m1fn).view(np.uint8) & 0xF
        words = (c[..., 0::2] | (c[..., 1::2] << 4)).reshape(k // 512, 128, 2 * n)
    return np.ascontiguousarray(words), np.ascontiguousarray(byte.astype(np.uint8).reshape(k // 512, 16, n))


def unpack_weight(words, scales, fmt):
    g, _, n = scales.shape
    words = np.ascontiguousarray(words).reshape(g, 128, n, -1)
    if fmt == "e4m3":
        vals = words.view(ml_dtypes.float8_e4m3fn).astype(np.float64)
    else:
        nib = np.empty((g, 128, n, 4), np.uint8)
        nib[..., 0::2] = words & 0xF
        nib[..., 1::2] = words >> 4
        vals = E2M1[nib]
    vals = vals * np.repeat(np.exp2(scales.astype(np.float64) - 127.0), 8, axis=1)[..., None]
    return vals.transpose(0, 1, 3, 2).reshape(g * 512, n)


def gelu(v):
    return 0.5 * v * (1.0 + np.tanh(np.sqrt(2.0 / np.pi) * (v + 0.044715 * v**3)))


def bf(x):
    return np.asarray(x, np.float32).astype(ml_dtypes.bfloat16)


def planes(Y):
    n, m = Y.shape
    b = f64(bf(Y)).reshape(n // 32, 32, m)
    amax = np.abs(b).max(1)
    byte = np.clip(np.where(amax > 0, np.frexp(amax)[1] - 1 + 127 - 7, 1), 1, 254)
    codes = (b * np.exp2(127.0 - byte)[:, None, :]).reshape(n, m).astype(np.float32).astype(ml_dtypes.float8_e4m3fn).view(np.uint8)
    words = codes.reshape(n // 512, 128, 4, m).transpose(0, 1, 3, 2)
    return np.ascontiguousarray(words), np.ascontiguousarray(byte.astype(np.uint8).reshape(n // 512, 16, m))


K, M, H, N, T, TM, S, T2, P = 1024, 512, 1024, 512, 2048, 1024, 512, 2048, 1024

def setup_inputs():
    n = np.random.standard_normal
    s, s2, u = mx_kscale(K)[:, None], mx_kscale(M)[:, None], mx_kscale(H)[:, None]
    perm = np.random.permutation(T2)
    d = {}
    d["tab_words"], d["tab_scales"] = pack_weight(n((K, T)) * s, "e4m3")
    d["tab2_words"], d["tab2_scales"] = pack_weight(n((M, TM)) * s2, "e4m3")
    d["offs"] = striped(np.random.permutation(T)[:S])
    d["offs2"] = striped(np.random.permutation(TM)[:S])
    d["offs3"] = striped(perm[:S])
    d["offs4"] = striped(perm[S:2 * S])
    d["offs5"] = striped(np.random.permutation(T2)[:P])
    d["w1"] = (n((K, H)) / K ** 0.5 / s).astype(np.float32)
    d["b1"] = (0.7 * n(H)).astype(np.float32)
    d["w2_words"], d["w2_scales"] = pack_weight(1.2 * n((M, H)) / M ** 0.5 / s2, "e4m3")
    d["w3"] = (1.2 * n((M, H)) / M ** 0.5 / s2).astype(np.float32)
    d["wg1"] = np.exp(0.3 * n((128, S))).astype(np.float32)
    d["wg2"] = np.exp(0.3 * n((128, S))).astype(np.float32)
    d["page0"] = (1.2 * n((H, T2))).astype(np.float32)
    d["gain"] = (np.exp(0.3 * n(H)) * u[:, 0]).astype(np.float32)
    d["w4_words"], d["w4_scales"] = pack_weight(n((H, N)) * np.exp(0.8 * n(N)) / H ** 0.5 / u, "e2m1")
    return d

def reference(tab_words, tab_scales, tab2_words, tab2_scales, offs, offs2, offs3, offs4, offs5,
              w1, b1, w2_words, w2_scales, w3, wg1, wg2, page0, gain, w4_words, w4_scales):
    v = unpack_weight(tab_words, tab_scales, "e4m3")[:, unstriped(offs)]
    v2 = unpack_weight(tab2_words, tab2_scales, "e4m3")[:, unstriped(offs2)]
    h1 = (mxq(f64(w1), 0, "e4m3").T @ v) + f64(b1)[:, None]
    e2 = unpack_weight(w2_words, w2_scales, "e4m3").T @ v2
    e3 = mxq(f64(w3), 0, "e4m3").T @ v2
    h2 = np.maximum(e2, e3)
    page = f64(page0).copy()
    page[:, unstriped(offs3)] = np.tile(f64(wg1), (H // 128, 1)) * h1
    page[:, unstriped(offs4)] = np.tile(f64(wg2), (H // 128, 1)) * h2
    x = f64(gain)[:, None] * np.tanh(page[:, unstriped(offs5)])
    y = unpack_weight(w4_words, w4_scales, "e2m1").T @ mxq(x, 0, "e4m3")
    words, scales = planes(y)
    return y, words, scales

@@ -1,0 +1,330 @@
+from contextlib import ExitStack
+
+import concourse.mybir as mybir
+
+K, M, H, N, T, TM, S, T2, R = 1024, 512, 1024, 512, 2048, 1024, 512, 2048, 1024
+FLOPS = 2 * (K * H * S + 2 * M * H * S + H * N * R)
+
+F32 = mybir.dt.float32
+BF16 = mybir.dt.bfloat16
+I32 = mybir.dt.int32
+U32 = mybir.dt.uint32
+U16 = mybir.dt.uint16
+U8 = mybir.dt.uint8
+FP8X4 = mybir.dt.float8_e4m3fn_x4
+FP4X4 = mybir.dt.float4_e2m1fn_x4
+ALU = mybir.AluOpType
+ACT = mybir.ActivationFunctionType
+
+P = 128
+PACK = 4
+PASS = P * PACK
+QUADS = 4
+CHUNK = 256
+YCOLS = 128
+PAGE_SLOT = [[1, 2, 5, 8], [3, 4, 1, 2]]
+H2_SLOT = [5, 8, 3, 4]
+Y_SLOT = [0, 6, 8, 3, 1, 5, 4, 2]
+VECTOR_BANKS = (1, 3, 5)
+Y_BANK = [0, 1, 6, 7, 2, 3, 4, 5]
+
+
+def tile_list_ring_advance_features_kernel(
+    tc, tab_words, tab_scales, tab2_words, tab2_scales, offs, offs2, offs3, offs4, offs5,
+    w1, b1, w2_words, w2_scales, w3, wg1, wg2, page0, gain, w4_words, w4_scales,
+    out_0, out_1, out_2,
+):
+    nc = tc.nc
+    with ExitStack() as ctx:
+        lists = ctx.enter_context(tc.tile_pool(name="lists", bufs=1))
+        keep = ctx.enter_context(tc.tile_pool(name="keep", bufs=1))
+        ring = ctx.enter_context(tc.tile_pool(name="ring", bufs=2))
+        psum = ctx.enter_context(tc.psum_pool(name="psum", bufs=1))
+
+        def kept(name, shape, dtype, tag=None, bufs=1):
+            return keep.tile(shape, dtype, name=name, tag=tag or name, bufs=bufs, align_bytes=64)
+
+        def load_list(name, source):
+            tile = lists.tile(list(source.shape), U16, name=name)
+            nc.sync.dma_start(tile[:], source)
+            return tile
+
+        def load_big(name, source, dtype, slot):
+            tile = keep.tile(list(source.shape), dtype, name=name, tag=f"slot{slot}", align_bytes=64)
+            nc.sync.dma_start(tile[:], source)
+            return tile
+
+        def words_of(words, a):
+            return words[a].rearrange("p c i -> p (c i)").bitcast(I32)
+
+        def weight_block(w, a, b):
+            return w[a * PASS:(a + 1) * PASS, b * PASS:(b + 1) * PASS].rearrange("(p i) c -> p i c", i=PACK)
+
+        def page_rows(b, t):
+            return page0[b * PASS:(b + 1) * PASS, :].rearrange("(p t) c -> p t c", t=PACK)[:, t, :]
+
+        def load_gate(tile, wg, first, quads):
+            for quad in quads:
+                nc.sync.dma_start(tile[32 * quad:32 * quad + 32, :, :],
+                                  wg.rearrange("(q t) j -> q t j", t=PACK)[:, first:first + 2, :])
+
+        gate_tiles = {name: kept(name, [P, 2, S], F32) for name in ("gate1a", "gate1b", "gate2a", "gate2b")}
+        gate1 = [gate_tiles["gate1" + "ab"[t // 2]][:, t % 2, :] for t in range(PACK)]
+        gate2 = [gate_tiles["gate2" + "ab"[t // 2]][:, t % 2, :] for t in range(PACK)]
+
+        tab2_s = kept("tab2_s", [P, TM], U8)
+        w2_s = kept("w2_s", [P, H], U8)
+        tab_s = kept("tab_s", [P, T], U8)
+        w4_s = kept("w4_s", [P, 2, N], U8)
+        for tile in (tab_s, w4_s):
+            nc.gpsimd.memset(tile[:].bitcast(I32), 0)
+
+        idx2 = load_list("idx2", offs2)
+        tab2_w = kept("tab2_w", [P, TM], I32)
+        nc.sync.dma_start(tab2_w[:], words_of(tab2_words, 0))
+        for quad in range(QUADS):
+            nc.sync.dma_start(tab2_s[32 * quad:32 * quad + 32, :].bitcast(I32),
+                              tab2_scales[0, 4 * quad:4 * quad + 4, :].bitcast(I32).unsqueeze(0).to_broadcast([8, 4, TM // 4]))
+        w3_raw, w1_raw, w2_w, page = {}, {}, {}, {}
+
+        def load_w2(b):
+            w2_w[b] = kept(f"w2_w{b}", [P, PASS], I32)
+            nc.sync.dma_start(w2_w[b][:], words_of(w2_words, 0)[:, b * PASS:(b + 1) * PASS])
+
+        def load_page(b, t):
+            page[b, t] = load_big(f"page{b}{t}", page_rows(b, t), F32, PAGE_SLOT[b][t])
+
+        w3_raw[0] = load_big("w3_raw0", weight_block(w3, 0, 0), F32, 0)
+        load_w2(0)
+        for quad in range(QUADS):
+            nc.sync.dma_start(w2_s[32 * quad:32 * quad + 32, :].bitcast(I32),
+                              w2_scales[0, 4 * quad:4 * quad + 4, :].bitcast(I32).unsqueeze(0).to_broadcast([8, 4, H // 4]))
+        idx4 = load_list("idx4", offs4)
+        load_page(0, 0)
+        load_gate(gate_tiles["gate2a"], wg2, 0, range(QUADS))
+        load_page(0, 1)
+        load_gate(gate_tiles["gate2b"], wg2, 2, range(QUADS))
+        load_page(0, 2)
+        load_page(0, 3)
+        idx = load_list("idx", offs)
+        tab_w = [load_big("tab_w0", words_of(tab_words, 0), I32, 3)]
+        for quad in range(QUADS):
+            nc.sync.dma_start(tab_s[32 * quad:32 * quad + 8, :].bitcast(I32),
+                              tab_scales[:, 4 * quad:4 * quad + 4, :].bitcast(I32))
+        tab_w.append(load_big("tab_w1", words_of(tab_words, 1), I32, 4))
+        w1_raw[0, 0] = load_big("w1_raw00", weight_block(w1, 0, 0), F32, 6)
+        bias = kept("bias", [P, 2, PACK], F32)
+        gains = kept("gains", [P, 2, PACK], F32)
+        nc.sync.dma_start(bias[:], b1.rearrange("(b p t) -> p b t", b=2, t=PACK))
+        nc.sync.dma_start(gains[:], gain.rearrange("(b p t) -> p b t", b=2, t=PACK))
+        w1_raw[1, 0] = load_big("w1_raw10", weight_block(w1, 1, 0), F32, 7)
+        idx3 = load_list("idx3", offs3)
+        load_gate(gate_tiles["gate1a"], wg1, 0, (0, 1))
+        w4_w = kept("w4_w", [P, 2, 2 * N], U8)
+        nc.sync.dma_start(w4_w[:].bitcast(I32), w4_words.rearrange("a p c -> p a c").bitcast(I32))
+        for quad in range(QUADS):
+            nc.sync.dma_start(w4_s[32 * quad:32 * quad + 4, :, :].bitcast(I32),
+                              w4_scales[:, 4 * quad:4 * quad + 4, :].rearrange("a r n -> r a n").bitcast(I32))
+        load_w2(1)
+        load_gate(gate_tiles["gate1a"], wg1, 0, (2, 3))
+        idx5 = load_list("idx5", offs5)
+        w3_raw[1] = load_big("w3_raw1", weight_block(w3, 0, 1), F32, 0)
+        w1_raw[0, 1] = load_big("w1_raw01", weight_block(w1, 0, 1), F32, 6)
+        w1_raw[1, 1] = load_big("w1_raw11", weight_block(w1, 1, 1), F32, 7)
+        load_gate(gate_tiles["gate1b"], wg1, 2, range(QUADS))
+        for t in range(PACK):
+            load_page(1, t)
+
+        def gather(out, window, offsets):
+            nc.vector.tensor_copy(out, window.indirect(offsets))
+
+        def round_weights(copy, raw, first, count):
+            rounded = ring.tile([P, count, P, PACK], BF16, name="rounded", tag="rounded", bufs=3, align_bytes=64)
+            copy(rounded[:].rearrange("p t q i -> p q i t"),
+                 raw[:].rearrange("p i (q t) -> p q i t", t=PACK)[:, :, :, first:first + count])
+            return rounded
+
+        def quantise(codes, scales, rounded):
+            nc.vector.quantize_mx(out=codes.bitcast(FP8X4), scales=scales, in_=rounded)
+
+        def round_shares(raw, shares):
+            return [(round_weights(copy, raw, first, count), first, count) for copy, first, count in shares]
+
+        def quantise_weights(name, rounded, tag=None):
+            codes = kept(name + "_codes", [P, PASS], U32, tag)
+            scales = kept(name + "_scales", [P, PASS], U8)
+            for tile, first, count in rounded:
+                cols = slice(first * P, (first + count) * P)
+                quantise(codes[:, cols], scales[:, cols], tile[:].rearrange("p t q i -> p (t q i)"))
+            return codes, scales
+
+        def deal_w2(b):
+            codes = kept(f"w2_codes{b}", [P, PASS], I32)
+            scales = kept(f"w2_scales{b}", [P, PASS], U8)
+            nc.vector.tensor_copy(codes[:].rearrange("p (t q) -> p q t", t=PACK),
+                                  w2_w[b][:].rearrange("p (q t) -> p q t", t=PACK))
+            nc.vector.tensor_copy(scales[:].rearrange("p (t q) -> p q t", t=PACK),
+                                  w2_s[:, b * PASS:(b + 1) * PASS].rearrange("p (q t) -> p q t", t=PACK))
+            return codes, scales
+
+        def bank(number, shape):
+            return psum.tile(shape, F32, name=f"bank{number}", tag=f"bank{number}")
+
+        def product(out, weights, t, moving, moving_scales, start, stop):
+            codes, scales = weights
+            cols = slice(t * P, (t + 1) * P)
+            nc.tensor.matmul_mx(out=out, lhsT=codes[:, cols].bitcast(FP8X4), lhsT_scale=scales[:, cols],
+                                rhs=moving.bitcast(FP8X4), rhs_scale=moving_scales, start=start, stop=stop)
+
+        v2_w = kept("v2_w", [P, S], U32)
+        v2_s = kept("v2_s", [P, S], U8)
+        gather(v2_w[:], tab2_w[:].bitcast(U32), idx2[:])
+        gather(v2_s[:], tab2_s[:], idx2[:])
+
+        h1, h2, e23 = {}, {}, {}
+
+        def soil_features(b, w2_q, w3_q):
+            for t in range(PACK):
+                e3_bank = bank(t % 2, [P, S])
+                product(e3_bank[:], w3_q, t, v2_w[:], v2_s[:], True, True)
+                e2_bank = bank(2 + t, [P, S])
+                product(e2_bank[:], w2_q, t, v2_w[:], v2_s[:], True, True)
+                e3 = ring.tile([P, S], F32, name="e3", tag="e3", bufs=4)
+                nc.scalar.copy(e3[:], e3_bank[:])
+                e23[b, t] = (e2_bank, e3)
+
+        def larger(b, t):
+            if b == 0:
+                h2[b, t] = kept("h2", [P, S], F32, bufs=2)
+            else:
+                h2[b, t] = kept(f"h2_1{t}", [P, S], F32, [None, "slot8", "x_bf00", "x_bf00"][t])
+            nc.vector.tensor_tensor(h2[b, t][:], e23[b, t][0][:], e23[b, t][1][:], ALU.max)
+
+        def cutter_features(b, w1_q):
+            for t in range(PACK):
+                acc = bank(6 + t % 2, [P, S])
+                for a in range(2):
+                    product(acc[:], w1_q[a], t, v_w[a][:], v_s[4 * a:P, :], a == 0, a == 1)
+                h1[b, t] = kept(f"h1_{b}{t}", [P, S], F32)
+                nc.scalar.activation(h1[b, t][:], acc[:], ACT.Identity, bias=bias[:, b, t:t + 1])
+
+        def put(b, t, offsets, values, gate):
+            nc.vector.tensor_tensor(page[b, t][:].indirect(offsets[:]), values[:], gate[t], ALU.mult)
+
+        x_bf = [[kept(f"x_bf0{c}", [P, R // 2, PACK], BF16) for c in range(2)],
+                [kept(f"x_bf1{c}", [P, CHUNK, PACK], BF16) for c in range(R // CHUNK)]]
+        x_codes, x_scales = {}, {}
+
+        def read_slots(b, t, first, count):
+            if (b, t) == (1, 1):
+                picked = kept("picked11", [P, R], F32, "x_bf01")
+            else:
+                picked = ring.tile([P, count], F32, name="picked", tag=f"picked{count}", bufs=4)
+            gather(picked[:], page[b, t][:], idx5[:, first // 16:(first + count) // 16])
+            if count == R:
+                squashed = keep.tile([P, R], F32, name="squashed", tag="slot7", align_bytes=64)[:]
+            else:
+                squashed = last_squashed[:, first:first + count]
+            nc.scalar.activation(squashed, picked[:], ACT.Tanh)
+            width = R // len(x_bf[b])
+            for j in range(0, count, width):
+                nc.scalar.activation(x_bf[b][(first + j) // width][:, :, t], squashed[:, j:j + width], ACT.Copy,
+                                     scale=gains[:, b, t:t + 1])
+
+        def quantise_x(b, first, count):
+            codes = kept(f"x_codes{b}{first}", [P, count], U32)
+            rounded = x_bf[b][first // count][:]
+            scales = kept(f"x_scales{b}{first}", [P, count], U8)
+            quantise(codes[:], scales[:], rounded.rearrange("p j t -> p (j t)"))
+            for j in range(0, count, YCOLS):
+                x_codes[b, (first + j) // YCOLS] = codes[:, j:j + YCOLS]
+                x_scales[b, (first + j) // YCOLS] = scales[:, j:j + YCOLS]
+
+        w3_q = quantise_weights("w3_0", round_shares(w3_raw[0], [(nc.vector.tensor_copy, 0, 2), (nc.scalar.copy, 2, 2)]))
+        soil_features(0, deal_w2(0), w3_q)
+        larger(0, 0)
+        larger(0, 1)
+        put(0, 0, idx4, h2[0, 0], gate2)
+        larger(0, 2)
+
+        put(0, 1, idx4, h2[0, 1], gate2)
+        larger(0, 3)
+        put(0, 2, idx4, h2[0, 2], gate2)
+        put(0, 3, idx4, h2[0, 3], gate2)
+        v_w = [kept(f"v_w{a}", [P, S], U32) for a in range(2)]
+        v_s = kept("v_s", [P, S], U8)
+        gather(v_w[0][:], tab_w[0][:].bitcast(U32), idx[:])
+        gather(v_s[:], tab_s[:], idx[:])
+        gather(v_w[1][:], tab_w[1][:].bitcast(U32), idx[:])
+        whole = [(nc.scalar.copy, 0, PACK)]
+        w1_q = [quantise_weights(f"w1_{a}0", round_shares(w1_raw[a, 0], whole)) for a in range(2)]
+        cutter_features(0, w1_q)
+
+        w4_codes = kept("w4_codes", [P, 2 * 2 * N], U8)
+        w4_sc = kept("w4_sc", [P, 2 * N], U8)
+        nc.vector.tensor_copy(w4_codes[:].bitcast(U16).rearrange("p (a t q) -> p a q t", a=2, t=PACK),
+                              w4_w[:].bitcast(U16).rearrange("p a (q t) -> p a q t", t=PACK))
+        nc.vector.tensor_copy(w4_sc[:].rearrange("p (a t q) -> p a q t", a=2, t=PACK),
+                              w4_s[:].rearrange("p a (q t) -> p a q t", t=PACK))
+
+        w2_q = deal_w2(1)
+        w3_bf = round_shares(w3_raw[1], whole)
+        w1_bf = [round_shares(w1_raw[a, 1], whole) for a in range(2)]
+        for t in range(PACK):
+            put(0, t, idx3, h1[0, t], gate1)
+            if t == 1:
+                soil_features(1, w2_q, quantise_weights("w3_1", w3_bf, "h1_03"))
+                cutter_features(1, [quantise_weights(f"w1_{a}1", w1_bf[a], [None, "slot5"][a]) for a in range(2)])
+            read_slots(0, t, 0, R)
+
+        for t in range(PACK):
+            if t == 0:
+                larger(1, t)
+            put(1, t, idx4, h2[1, t], gate2)
+            put(1, t, idx3, h1[1, t], gate1)
+            if t < PACK - 1:
+                if t == 1:
+                    quantise_x(0, 0, R // 2)
+                    quantise_x(0, R // 2, R // 2)
+                larger(1, t + 1)
+                read_slots(1, t, 0, R)
+
+
+        def last_product(acc, c, a):
+            for t in range(PACK):
+                n0 = (a * PACK + t) * P
+                nc.tensor.matmul_mx(out=acc[:, t, :], lhsT=w4_codes[:, 2 * n0:2 * n0 + 2 * P].bitcast(FP4X4),
+                                    lhsT_scale=w4_sc[:, n0:n0 + P],
+                                    rhs=x_codes[a, c].bitcast(FP8X4), rhs_scale=x_scales[a, c],
+                                    start=(a == 0 and t == 0), stop=(a == 1 and t == PACK - 1))
+
+        y_banks = [bank(Y_BANK[c], [P, PACK, YCOLS]) for c in range(R // YCOLS)]
+        for c in range(R // YCOLS):
+            last_product(y_banks[c], c, 0)
+
+        last_squashed = keep.tile([P, R], F32, name="squashed", tag="slot7", align_bytes=64)
+        y_codes = kept("y_codes", [P, R], U32)
+        y_scales = kept("y_scales", [P, R], U8)
+        y_rows = out_0.rearrange("(p t) j -> p t j", t=PACK)
+        y_words = words_of(out_1, 0)
+        for first in range(0, R, CHUNK):
+            cols = slice(first, first + CHUNK)
+            read_slots(1, PACK - 1, first, CHUNK)
+            quantise_x(1, first, CHUNK)
+            y_bf = ring.tile([P, CHUNK, PACK], BF16, name="y_bf", tag="rounded", bufs=3, align_bytes=64)
+            for part in range(CHUNK // YCOLS):
+                c = first // YCOLS + part
+                last_product(y_banks[c], c, 1)
+                y = keep.tile([P, PACK, YCOLS], F32, name="y", tag=f"slot{Y_SLOT[c]}", align_bytes=64)
+                copy = nc.vector.tensor_copy if c in VECTOR_BANKS else nc.scalar.copy
+                copy(y[:], y_banks[c][:])
+                nc.sync.dma_start(y_rows[:, :, c * YCOLS:(c + 1) * YCOLS], y[:])
+                nc.vector.tensor_copy(
+                    y_bf[:, part * YCOLS:(part + 1) * YCOLS, :].rearrange("p (c i) t -> p c t i", i=4),
+                    y[:].rearrange("p t (c i) -> p c t i", i=4))
+            quantise(y_codes[:, cols], y_scales[:, cols], y_bf[:].rearrange("p j t -> p (j t)"))
+            nc.sync.dma_start(y_words[:, cols], y_codes[:, cols].bitcast(I32))
+        for quad in range(QUADS):
+            queue = nc.scalar if quad % 2 else nc.sync
+            queue.dma_start(out_2[0, 4 * quad:4 * quad + 4, :].bitcast(I32),
+                            y_scales[32 * quad:32 * quad + 4, :].bitcast(I32))

@@ -101,9 +101,9 @@ def tile_list_ring_advance_features_kernel(
                               w2_scales[0, 4 * quad:4 * quad + 4, :].bitcast(I32).unsqueeze(0).to_broadcast([8, 4, H // 4]))
         idx4 = load_list("idx4", offs4)
         load_page(0, 0)
-        load_gate(gate_tiles["gate2a"], wg2, 0, range(QUADS))
+        load_gate(gate_tiles["gate2a"], wg2, 0, (0, 2, 1, 3))
         load_page(0, 1)
-        load_gate(gate_tiles["gate2b"], wg2, 2, range(QUADS))
+        load_gate(gate_tiles["gate2b"], wg2, 2, (0, 2, 1, 3))
         load_page(0, 2)
         load_page(0, 3)
         idx = load_list("idx", offs)
@@ -119,19 +119,19 @@ def tile_list_ring_advance_features_kernel(
         nc.sync.dma_start(gains[:], gain.rearrange("(b p t) -> p b t", b=2, t=PACK))
         w1_raw[1, 0] = load_big("w1_raw10", weight_block(w1, 1, 0), F32, 7)
         idx3 = load_list("idx3", offs3)
-        load_gate(gate_tiles["gate1a"], wg1, 0, (0, 1))
+        load_gate(gate_tiles["gate1a"], wg1, 0, (0, 2))
         w4_w = kept("w4_w", [P, 2, 2 * N], U8)
         nc.sync.dma_start(w4_w[:].bitcast(I32), w4_words.rearrange("a p c -> p a c").bitcast(I32))
         for quad in range(QUADS):
             nc.sync.dma_start(w4_s[32 * quad:32 * quad + 4, :, :].bitcast(I32),
                               w4_scales[:, 4 * quad:4 * quad + 4, :].rearrange("a r n -> r a n").bitcast(I32))
         load_w2(1)
-        load_gate(gate_tiles["gate1a"], wg1, 0, (2, 3))
+        load_gate(gate_tiles["gate1a"], wg1, 0, (1, 3))
         idx5 = load_list("idx5", offs5)
         w3_raw[1] = load_big("w3_raw1", weight_block(w3, 0, 1), F32, 0)
         w1_raw[0, 1] = load_big("w1_raw01", weight_block(w1, 0, 1), F32, 6)
         w1_raw[1, 1] = load_big("w1_raw11", weight_block(w1, 1, 1), F32, 7)
-        load_gate(gate_tiles["gate1b"], wg1, 2, range(QUADS))
+        load_gate(gate_tiles["gate1b"], wg1, 2, (0, 2, 1, 3))
         for t in range(PACK):
             load_page(1, t)
 
@@ -140,8 +140,8 @@ def tile_list_ring_advance_features_kernel(
 
         def round_weights(copy, raw, first, count):
             rounded = ring.tile([P, count, P, PACK], BF16, name="rounded", tag="rounded", bufs=3, align_bytes=64)
-            copy(rounded[:].rearrange("p t q i -> p q i t"),
-                 raw[:].rearrange("p i (q t) -> p q i t", t=PACK)[:, :, :, first:first + count])
+            copy(rounded[:].rearrange("p (u e) q i -> p u q i e", e=2),
+                 raw[:].rearrange("p i (q u e) -> p u q i e", u=2, e=2)[:, first // 2:(first + count) // 2])
             return rounded
 
         def quantise(codes, scales, rounded):
@@ -161,10 +161,10 @@ def tile_list_ring_advance_features_kernel(
         def deal_w2(b):
             codes = kept(f"w2_codes{b}", [P, PASS], I32)
             scales = kept(f"w2_scales{b}", [P, PASS], U8)
-            nc.vector.tensor_copy(codes[:].rearrange("p (t q) -> p q t", t=PACK),
-                                  w2_w[b][:].rearrange("p (q t) -> p q t", t=PACK))
-            nc.vector.tensor_copy(scales[:].rearrange("p (t q) -> p q t", t=PACK),
-                                  w2_s[:, b * PASS:(b + 1) * PASS].rearrange("p (q t) -> p q t", t=PACK))
+            nc.vector.tensor_copy(codes[:].rearrange("p (u e q) -> p u q e", u=2, e=2),
+                                  w2_w[b][:].rearrange("p (q u e) -> p u q e", u=2, e=2))
+            nc.vector.tensor_copy(scales[:].rearrange("p (t q) -> p t q", t=PACK),
+                                  w2_s[:, b * PASS:(b + 1) * PASS].rearrange("p (q t) -> p t q", t=PACK))
             return codes, scales
 
         def bank(number, shape):
@@ -262,10 +262,10 @@ def tile_list_ring_advance_features_kernel(
 
         w4_codes = kept("w4_codes", [P, 2 * 2 * N], U8)
         w4_sc = kept("w4_sc", [P, 2 * N], U8)
-        nc.vector.tensor_copy(w4_codes[:].bitcast(U16).rearrange("p (a t q) -> p a q t", a=2, t=PACK),
-                              w4_w[:].bitcast(U16).rearrange("p a (q t) -> p a q t", t=PACK))
-        nc.vector.tensor_copy(w4_sc[:].rearrange("p (a t q) -> p a q t", a=2, t=PACK),
-                              w4_s[:].rearrange("p a (q t) -> p a q t", t=PACK))
+        nc.vector.tensor_copy(w4_codes[:].bitcast(U16).rearrange("p (a t q) -> p a t q", a=2, t=PACK),
+                              w4_w[:].bitcast(U16).rearrange("p a (q t) -> p a t q", t=PACK))
+        nc.vector.tensor_copy(w4_sc[:].rearrange("p (a t q) -> p a t q", a=2, t=PACK),
+                              w4_s[:].rearrange("p a (q t) -> p a t q", t=PACK))
 
         w2_q = deal_w2(1)
         w3_bf = round_shares(w3_raw[1], whole)
@@ -320,8 +320,8 @@ def tile_list_ring_advance_features_kernel(
                 copy(y[:], y_banks[c][:])
                 nc.sync.dma_start(y_rows[:, :, c * YCOLS:(c + 1) * YCOLS], y[:])
                 nc.vector.tensor_copy(
-                    y_bf[:, part * YCOLS:(part + 1) * YCOLS, :].rearrange("p (c i) t -> p c t i", i=4),
-                    y[:].rearrange("p t (c i) -> p c t i", i=4))
+                    y_bf[:, part * YCOLS:(part + 1) * YCOLS, :].rearrange("p (c i) t -> p c t i", i=2),
+                    y[:].rearrange("p t (c i) -> p c t i", i=2))
             quantise(y_codes[:, cols], y_scales[:, cols], y_bf[:].rearrange("p j t -> p (j t)"))
             nc.sync.dma_start(y_words[:, cols], y_codes[:, cols].bitcast(I32))
         for quad in range(QUADS):

@@ -1,6 +1,7 @@
 from contextlib import ExitStack
 
 import concourse.mybir as mybir
+from concourse.masks import make_identity
 
 K, M, H, N, T, TM, S, T2, R = 1024, 512, 1024, 512, 2048, 1024, 512, 2048, 1024
 FLOPS = 2 * (K * H * S + 2 * M * H * S + H * N * R)
@@ -22,10 +23,13 @@ PASS = P * PACK
 QUADS = 4
 CHUNK = 256
 YCOLS = 128
-PAGE_SLOT = [[1, 2, 5, 8], [3, 4, 1, 2]]
+PICKED_TAG = [["pickedA", "pickedB", "pickedB", "pickedB"], ["pickedA", "x_bf01", "pickedB"]]
+PAGE_SLOT = [[1, 2, 5, 8], [3, 9, 0, 4]]
 H2_SLOT = [5, 8, 3, 4]
-Y_SLOT = [0, 6, 8, 3, 1, 5, 4, 2]
-VECTOR_BANKS = (1, 3, 5)
+Y_SLOT = [1, 2, 6, 8]
+VECTOR_BANKS = ()
+HELD = {}
+WORD_STORES = {512: 0, 1024: 512}
 Y_BANK = [0, 1, 6, 7, 2, 3, 4, 5]
 
 
@@ -63,28 +67,23 @@ def tile_list_ring_advance_features_kernel(
         def page_rows(b, t):
             return page0[b * PASS:(b + 1) * PASS, :].rearrange("(p t) c -> p t c", t=PACK)[:, t, :]
 
-        def load_gate(tile, wg, first, quads):
-            for quad in quads:
-                nc.sync.dma_start(tile[32 * quad:32 * quad + 32, :, :],
-                                  wg.rearrange("(q t) j -> q t j", t=PACK)[:, first:first + 2, :])
+        def load_gate(name, wg):
+            tile = kept(name, [P, S], F32)
+            nc.sync.dma_start(tile[:], wg)
+            return tile
 
-        gate_tiles = {name: kept(name, [P, 2, S], F32) for name in ("gate1a", "gate1b", "gate2a", "gate2b")}
-        gate1 = [gate_tiles["gate1" + "ab"[t // 2]][:, t % 2, :] for t in range(PACK)]
-        gate2 = [gate_tiles["gate2" + "ab"[t // 2]][:, t % 2, :] for t in range(PACK)]
 
         tab2_s = kept("tab2_s", [P, TM], U8)
         w2_s = kept("w2_s", [P, H], U8)
         tab_s = kept("tab_s", [P, T], U8)
         w4_s = kept("w4_s", [P, 2, N], U8)
-        for tile in (tab_s, w4_s):
+
+        identity = kept("identity", [P, P], F32)
+        nc.gpsimd.memset(tab2_s[:].bitcast(I32), 0)
+        make_identity(nc, identity[:])
+        for tile in (w2_s, tab_s, w4_s):
             nc.gpsimd.memset(tile[:].bitcast(I32), 0)
 
-        idx2 = load_list("idx2", offs2)
-        tab2_w = kept("tab2_w", [P, TM], I32)
-        nc.sync.dma_start(tab2_w[:], words_of(tab2_words, 0))
-        for quad in range(QUADS):
-            nc.sync.dma_start(tab2_s[32 * quad:32 * quad + 32, :].bitcast(I32),
-                              tab2_scales[0, 4 * quad:4 * quad + 4, :].bitcast(I32).unsqueeze(0).to_broadcast([8, 4, TM // 4]))
         w3_raw, w1_raw, w2_w, page = {}, {}, {}, {}
 
         def load_w2(b):
@@ -94,52 +93,61 @@ def tile_list_ring_advance_features_kernel(
         def load_page(b, t):
             page[b, t] = load_big(f"page{b}{t}", page_rows(b, t), F32, PAGE_SLOT[b][t])
 
+        def load_scale_rows(tile, scales):
+            for quad in range(QUADS):
+                nc.sync.dma_start(tile[32 * quad:32 * quad + 4, :].bitcast(I32),
+                                  scales[0, 4 * quad:4 * quad + 4, :].bitcast(I32))
+
+        wg2_rows = load_gate("wg2_rows", wg2)
+        idx2 = load_list("idx2", offs2)
+        tab2_w = kept("tab2_w", [P, TM], I32)
+        nc.sync.dma_start(tab2_w[:], words_of(tab2_words, 0))
+        load_scale_rows(tab2_s, tab2_scales)
         w3_raw[0] = load_big("w3_raw0", weight_block(w3, 0, 0), F32, 0)
         load_w2(0)
-        for quad in range(QUADS):
-            nc.sync.dma_start(w2_s[32 * quad:32 * quad + 32, :].bitcast(I32),
-                              w2_scales[0, 4 * quad:4 * quad + 4, :].bitcast(I32).unsqueeze(0).to_broadcast([8, 4, H // 4]))
+        load_scale_rows(w2_s, w2_scales)
         idx4 = load_list("idx4", offs4)
         load_page(0, 0)
-        load_gate(gate_tiles["gate2a"], wg2, 0, (0, 2, 1, 3))
         load_page(0, 1)
-        load_gate(gate_tiles["gate2b"], wg2, 2, (0, 2, 1, 3))
         load_page(0, 2)
+        w3_raw[1] = load_big("w3_raw1", weight_block(w3, 0, 1), F32, 0)
+        load_w2(1)
         load_page(0, 3)
+        load_page(1, 0)
+        load_page(1, 1)
+        wg1_rows = load_gate("wg1_rows", wg1)
         idx = load_list("idx", offs)
-        tab_w = [load_big("tab_w0", words_of(tab_words, 0), I32, 3)]
+        tab_w = [load_big("tab_w0", words_of(tab_words, 0), I32, 0)]
         for quad in range(QUADS):
             nc.sync.dma_start(tab_s[32 * quad:32 * quad + 8, :].bitcast(I32),
                               tab_scales[:, 4 * quad:4 * quad + 4, :].bitcast(I32))
         tab_w.append(load_big("tab_w1", words_of(tab_words, 1), I32, 4))
         w1_raw[0, 0] = load_big("w1_raw00", weight_block(w1, 0, 0), F32, 6)
+        w1_raw[1, 0] = load_big("w1_raw10", weight_block(w1, 1, 0), F32, 7)
         bias = kept("bias", [P, 2, PACK], F32)
         gains = kept("gains", [P, 2, PACK], F32)
         nc.sync.dma_start(bias[:], b1.rearrange("(b p t) -> p b t", b=2, t=PACK))
         nc.sync.dma_start(gains[:], gain.rearrange("(b p t) -> p b t", b=2, t=PACK))
-        w1_raw[1, 0] = load_big("w1_raw10", weight_block(w1, 1, 0), F32, 7)
         idx3 = load_list("idx3", offs3)
-        load_gate(gate_tiles["gate1a"], wg1, 0, (0, 2))
+        idx5 = load_list("idx5", offs5)
         w4_w = kept("w4_w", [P, 2, 2 * N], U8)
         nc.sync.dma_start(w4_w[:].bitcast(I32), w4_words.rearrange("a p c -> p a c").bitcast(I32))
         for quad in range(QUADS):
             nc.sync.dma_start(w4_s[32 * quad:32 * quad + 4, :, :].bitcast(I32),
                               w4_scales[:, 4 * quad:4 * quad + 4, :].rearrange("a r n -> r a n").bitcast(I32))
-        load_w2(1)
-        load_gate(gate_tiles["gate1a"], wg1, 0, (1, 3))
-        idx5 = load_list("idx5", offs5)
-        w3_raw[1] = load_big("w3_raw1", weight_block(w3, 0, 1), F32, 0)
         w1_raw[0, 1] = load_big("w1_raw01", weight_block(w1, 0, 1), F32, 6)
         w1_raw[1, 1] = load_big("w1_raw11", weight_block(w1, 1, 1), F32, 7)
-        load_gate(gate_tiles["gate1b"], wg1, 2, (0, 2, 1, 3))
-        for t in range(PACK):
-            load_page(1, t)
+        load_page(1, 2)
+        load_page(1, 3)
 
         def gather(out, window, offsets):
             nc.vector.tensor_copy(out, window.indirect(offsets))
 
-        def round_weights(copy, raw, first, count):
-            rounded = ring.tile([P, count, P, PACK], BF16, name="rounded", tag="rounded", bufs=3, align_bytes=64)
+        def round_weights(copy, raw, first, count, tag):
+            if tag is None:
+                rounded = ring.tile([P, count, P, PACK], BF16, name="rounded", tag="rounded", bufs=2, align_bytes=64)
+            else:
+                rounded = kept("rounded", [P, count, P, PACK], BF16, tag)
             copy(rounded[:].rearrange("p (u e) q i -> p u q i e", e=2),
                  raw[:].rearrange("p i (q u e) -> p u q i e", u=2, e=2)[:, first // 2:(first + count) // 2])
             return rounded
@@ -147,11 +155,12 @@ def tile_list_ring_advance_features_kernel(
         def quantise(codes, scales, rounded):
             nc.vector.quantize_mx(out=codes.bitcast(FP8X4), scales=scales, in_=rounded)
 
-        def round_shares(raw, shares):
-            return [(round_weights(copy, raw, first, count), first, count) for copy, first, count in shares]
+        def round_shares(raw, shares, tag=None):
+            return [(round_weights(copy, raw, first, count, tag), first, count) for copy, first, count in shares]
 
-        def quantise_weights(name, rounded, tag=None):
-            codes = kept(name + "_codes", [P, PASS], U32, tag)
+        def quantise_weights(name, rounded, codes=None):
+            if codes is None:
+                codes = kept(name + "_codes", [P, PASS], U32)[:]
             scales = kept(name + "_scales", [P, PASS], U8)
             for tile, first, count in rounded:
                 cols = slice(first * P, (first + count) * P)
@@ -176,6 +185,23 @@ def tile_list_ring_advance_features_kernel(
             nc.tensor.matmul_mx(out=out, lhsT=codes[:, cols].bitcast(FP8X4), lhsT_scale=scales[:, cols],
                                 rhs=moving.bitcast(FP8X4), rhs_scale=moving_scales, start=start, stop=stop)
 
+        def turn_gate(rows):
+            turned = bank(6, [P, PACK, P])
+            for c in range(S // P):
+                nc.tensor.transpose(turned[:, c, :], rows[:, c * P:(c + 1) * P], identity[:])
+            return turned
+
+        def deal_gate(name, turned, t):
+            columns = kept(f"columns{t % 2}", [P, S // P, QUADS, 32], F32)
+            nc.scalar.copy(columns[:], turned[:].rearrange("p c (q t) -> p c t q", t=PACK)[:, :, t:t + 1, :]
+                           .to_broadcast([P, S // P, QUADS, 32]))
+            dealt = bank(7 if t % 2 == 0 else 0, [P, S])
+            for c in range(S // P):
+                nc.tensor.transpose(dealt[:, c * P:(c + 1) * P], columns[:, c].rearrange("p a q -> p (a q)"), identity[:])
+            gate = kept(f"{name}_{t}", [P, S], F32)
+            nc.scalar.copy(gate[:], dealt[:])
+            return gate[:]
+
         v2_w = kept("v2_w", [P, S], U32)
         v2_s = kept("v2_s", [P, S], U8)
         gather(v2_w[:], tab2_w[:].bitcast(U32), idx2[:])
@@ -189,15 +215,18 @@ def tile_list_ring_advance_features_kernel(
                 product(e3_bank[:], w3_q, t, v2_w[:], v2_s[:], True, True)
                 e2_bank = bank(2 + t, [P, S])
                 product(e2_bank[:], w2_q, t, v2_w[:], v2_s[:], True, True)
-                e3 = ring.tile([P, S], F32, name="e3", tag="e3", bufs=4)
+                if b == 0 and t < 2:
+                    e3 = kept("e3", [P, S], F32, f"columns{1 - t}")
+                else:
+                    e3 = ring.tile([P, S], F32, name="e3", tag="e3", bufs=4)
                 nc.scalar.copy(e3[:], e3_bank[:])
                 e23[b, t] = (e2_bank, e3)
 
         def larger(b, t):
-            if b == 0:
+            if b == 0 or t < 2:
                 h2[b, t] = kept("h2", [P, S], F32, bufs=2)
             else:
-                h2[b, t] = kept(f"h2_1{t}", [P, S], F32, [None, "slot8", "x_bf00", "x_bf00"][t])
+                h2[b, t] = kept(f"h2_1{t}", [P, S], F32, "x_bf00")
             nc.vector.tensor_tensor(h2[b, t][:], e23[b, t][0][:], e23[b, t][1][:], ALU.max)
 
         def cutter_features(b, w1_q):
@@ -216,20 +245,27 @@ def tile_list_ring_advance_features_kernel(
         x_codes, x_scales = {}, {}
 
         def read_slots(b, t, first, count):
-            if (b, t) == (1, 1):
-                picked = kept("picked11", [P, R], F32, "x_bf01")
+            if count == R:
+                picked = kept(f"picked{b}{t}", [P, R], F32, PICKED_TAG[b][t])
             else:
-                picked = ring.tile([P, count], F32, name="picked", tag=f"picked{count}", bufs=4)
+                picked = ring.tile([P, count], F32, name="picked", tag=f"picked{count}", bufs=2)
             gather(picked[:], page[b, t][:], idx5[:, first // 16:(first + count) // 16])
             if count == R:
                 squashed = keep.tile([P, R], F32, name="squashed", tag="slot7", align_bytes=64)[:]
             else:
-                squashed = last_squashed[:, first:first + count]
+                c = first // CHUNK
+                if c in HELD:
+                    squashed = kept(f"squashed{c}", [P, count], F32, f"x_codes1{HELD[c] * CHUNK}")[:]
+                else:
+                    squashed = last_squashed[:, first:first + count]
             nc.scalar.activation(squashed, picked[:], ACT.Tanh)
             width = R // len(x_bf[b])
             for j in range(0, count, width):
-                nc.scalar.activation(x_bf[b][(first + j) // width][:, :, t], squashed[:, j:j + width], ACT.Copy,
-                                     scale=gains[:, b, t:t + 1])
+                plane = x_bf[b][(first + j) // width][:, :, t]
+                if count == R:
+                    nc.scalar.activation(plane, squashed[:, j:j + width], ACT.Copy, scale=gains[:, b, t:t + 1])
+                else:
+                    nc.vector.tensor_scalar(plane, squashed[:, j:j + width], gains[:, b, t:t + 1], None, ALU.mult)
 
         def quantise_x(b, first, count):
             codes = kept(f"x_codes{b}{first}", [P, count], U32)
@@ -240,8 +276,11 @@ def tile_list_ring_advance_features_kernel(
                 x_codes[b, (first + j) // YCOLS] = codes[:, j:j + YCOLS]
                 x_scales[b, (first + j) // YCOLS] = scales[:, j:j + YCOLS]
 
+        turned = turn_gate(wg2_rows)
+        gate2 = [deal_gate("gate2", turned, 0)]
         w3_q = quantise_weights("w3_0", round_shares(w3_raw[0], [(nc.vector.tensor_copy, 0, 2), (nc.scalar.copy, 2, 2)]))
         soil_features(0, deal_w2(0), w3_q)
+        gate2.extend(deal_gate("gate2", turned, t) for t in range(1, PACK))
         larger(0, 0)
         larger(0, 1)
         put(0, 0, idx4, h2[0, 0], gate2)
@@ -250,16 +289,21 @@ def tile_list_ring_advance_features_kernel(
         put(0, 1, idx4, h2[0, 1], gate2)
         larger(0, 3)
         put(0, 2, idx4, h2[0, 2], gate2)
+        whole = [(nc.scalar.copy, 0, PACK)]
+        soil_features(1, deal_w2(1), quantise_weights("w3_1", round_shares(w3_raw[1], whole)))
         put(0, 3, idx4, h2[0, 3], gate2)
+        for t in range(2):
+            larger(1, t)
+            put(1, t, idx4, h2[1, t], gate2)
+
+        turned = turn_gate(wg1_rows)
+        gate1 = [deal_gate("gate1", turned, t) for t in range(PACK)]
         v_w = [kept(f"v_w{a}", [P, S], U32) for a in range(2)]
         v_s = kept("v_s", [P, S], U8)
         gather(v_w[0][:], tab_w[0][:].bitcast(U32), idx[:])
         gather(v_s[:], tab_s[:], idx[:])
         gather(v_w[1][:], tab_w[1][:].bitcast(U32), idx[:])
-        whole = [(nc.scalar.copy, 0, PACK)]
-        w1_q = [quantise_weights(f"w1_{a}0", round_shares(w1_raw[a, 0], whole)) for a in range(2)]
-        cutter_features(0, w1_q)
-
+        cutter_features(0, [quantise_weights(f"w1_{a}0", round_shares(w1_raw[a, 0], whole, [None, "w4_codes"][a])) for a in range(2)])
         w4_codes = kept("w4_codes", [P, 2 * 2 * N], U8)
         w4_sc = kept("w4_sc", [P, 2 * N], U8)
         nc.vector.tensor_copy(w4_codes[:].bitcast(U16).rearrange("p (a t q) -> p a t q", a=2, t=PACK),
@@ -267,28 +311,25 @@ def tile_list_ring_advance_features_kernel(
         nc.vector.tensor_copy(w4_sc[:].rearrange("p (a t q) -> p a t q", a=2, t=PACK),
                               w4_s[:].rearrange("p a (q t) -> p a t q", t=PACK))
 
-        w2_q = deal_w2(1)
-        w3_bf = round_shares(w3_raw[1], whole)
         w1_bf = [round_shares(w1_raw[a, 1], whole) for a in range(2)]
         for t in range(PACK):
             put(0, t, idx3, h1[0, t], gate1)
-            if t == 1:
-                soil_features(1, w2_q, quantise_weights("w3_1", w3_bf, "h1_03"))
-                cutter_features(1, [quantise_weights(f"w1_{a}1", w1_bf[a], [None, "slot5"][a]) for a in range(2)])
+            if t == 2:
+                late_codes = kept("late_codes", [P, 2, PASS], U32, "slot5")
+                cutter_features(1, [quantise_weights(f"w1_{a}1", w1_bf[a], late_codes[:, a, :]) for a in range(2)])
             read_slots(0, t, 0, R)
 
         for t in range(PACK):
-            if t == 0:
-                larger(1, t)
-            put(1, t, idx4, h2[1, t], gate2)
+            if t >= 2:
+                put(1, t, idx4, h2[1, t], gate2)
             put(1, t, idx3, h1[1, t], gate1)
-            if t < PACK - 1:
-                if t == 1:
-                    quantise_x(0, 0, R // 2)
-                    quantise_x(0, R // 2, R // 2)
+            if t == 1:
+                quantise_x(0, 0, R // 2)
+                quantise_x(0, R // 2, R // 2)
+            if t in (1, 2):
                 larger(1, t + 1)
+            if t < PACK - 1:
                 read_slots(1, t, 0, R)
-
 
         def last_product(acc, c, a):
             for t in range(PACK):
@@ -311,19 +352,21 @@ def tile_list_ring_advance_features_kernel(
             cols = slice(first, first + CHUNK)
             read_slots(1, PACK - 1, first, CHUNK)
             quantise_x(1, first, CHUNK)
-            y_bf = ring.tile([P, CHUNK, PACK], BF16, name="y_bf", tag="rounded", bufs=3, align_bytes=64)
+            y = keep.tile([P, PACK, CHUNK], F32, name="y", tag=f"slot{Y_SLOT[first // CHUNK]}", align_bytes=64)
+            y_bf = ring.tile([P, CHUNK, PACK], BF16, name="y_bf", tag="rounded", bufs=2, align_bytes=64)
             for part in range(CHUNK // YCOLS):
                 c = first // YCOLS + part
                 last_product(y_banks[c], c, 1)
-                y = keep.tile([P, PACK, YCOLS], F32, name="y", tag=f"slot{Y_SLOT[c]}", align_bytes=64)
                 copy = nc.vector.tensor_copy if c in VECTOR_BANKS else nc.scalar.copy
-                copy(y[:], y_banks[c][:])
-                nc.sync.dma_start(y_rows[:, :, c * YCOLS:(c + 1) * YCOLS], y[:])
+                copy(y[:, :, part * YCOLS:(part + 1) * YCOLS], y_banks[c][:])
                 nc.vector.tensor_copy(
                     y_bf[:, part * YCOLS:(part + 1) * YCOLS, :].rearrange("p (c i) t -> p c t i", i=2),
-                    y[:].rearrange("p t (c i) -> p c t i", i=2))
+                    y[:, :, part * YCOLS:(part + 1) * YCOLS].rearrange("p t (c i) -> p c t i", i=2))
+            nc.sync.dma_start(y_rows[:, :, cols], y[:])
             quantise(y_codes[:, cols], y_scales[:, cols], y_bf[:].rearrange("p j t -> p (j t)"))
-            nc.sync.dma_start(y_words[:, cols], y_codes[:, cols].bitcast(I32))
+            if first + CHUNK in WORD_STORES:
+                done = slice(WORD_STORES[first + CHUNK], first + CHUNK)
+                nc.sync.dma_start(y_words[:, done], y_codes[:, done].bitcast(I32))
         for quad in range(QUADS):
             queue = nc.scalar if quad % 2 else nc.sync
             queue.dma_start(out_2[0, 4 * quad:4 * quad + 4, :].bitcast(I32),

@@ -3,7 +3,7 @@ from contextlib import ExitStack
 import concourse.mybir as mybir
 from concourse.masks import make_identity
 
-K, M, H, N, T, TM, S, T2, R = 1024, 512, 1024, 512, 2048, 1024, 512, 2048, 1024
+K, M, H, N, T, TM, S, R = 1024, 512, 1024, 512, 2048, 1024, 512, 1024
 FLOPS = 2 * (K * H * S + 2 * M * H * S + H * N * R)
 
 F32 = mybir.dt.float32
@@ -20,17 +20,13 @@ ACT = mybir.ActivationFunctionType
 P = 128
 PACK = 4
 PASS = P * PACK
-QUADS = 4
+QUAD = 32
+QUADS = P // QUAD
+LIST_ROWS = 16
+LAST = PACK - 1
 CHUNK = 256
-YCOLS = 128
-PICKED_TAG = [["pickedA", "pickedB", "pickedB", "pickedB"], ["pickedA", "x_bf01", "pickedB"]]
-PAGE_SLOT = [[1, 2, 5, 8], [3, 9, 0, 4]]
-H2_SLOT = [5, 8, 3, 4]
-Y_SLOT = [1, 2, 6, 8]
-VECTOR_BANKS = ()
-HELD = {}
-WORD_STORES = {512: 0, 1024: 512}
-Y_BANK = [0, 1, 6, 7, 2, 3, 4, 5]
+BANK_SLOTS = 128
+SCALAR_GAIN_CHUNK = 1
 
 
 def tile_list_ring_advance_features_kernel(
@@ -42,332 +38,296 @@ def tile_list_ring_advance_features_kernel(
     with ExitStack() as ctx:
         lists = ctx.enter_context(tc.tile_pool(name="lists", bufs=1))
         keep = ctx.enter_context(tc.tile_pool(name="keep", bufs=1))
-        ring = ctx.enter_context(tc.tile_pool(name="ring", bufs=2))
         psum = ctx.enter_context(tc.psum_pool(name="psum", bufs=1))
 
-        def kept(name, shape, dtype, tag=None, bufs=1):
+        def sbuf(name, shape, dtype, tag=None, bufs=1):
             return keep.tile(shape, dtype, name=name, tag=tag or name, bufs=bufs, align_bytes=64)
+
+        def bank(number, shape):
+            return psum.tile(shape, F32, name=f"bank{number}", tag=f"bank{number}")
+
+        def load(name, source, dtype, tag=None):
+            tile = sbuf(name, list(source.shape), dtype, tag)
+            nc.sync.dma_start(tile[:], source)
+            return tile
 
         def load_list(name, source):
             tile = lists.tile(list(source.shape), U16, name=name)
             nc.sync.dma_start(tile[:], source)
             return tile
 
-        def load_big(name, source, dtype, slot):
-            tile = keep.tile(list(source.shape), dtype, name=name, tag=f"slot{slot}", align_bytes=64)
-            nc.sync.dma_start(tile[:], source)
-            return tile
-
         def words_of(words, a):
             return words[a].rearrange("p c i -> p (c i)").bitcast(I32)
 
-        def weight_block(w, a, b):
-            return w[a * PASS:(a + 1) * PASS, b * PASS:(b + 1) * PASS].rearrange("(p i) c -> p i c", i=PACK)
+        def load_weight(name, w, a, b, tag):
+            block = w[a * PASS:(a + 1) * PASS, b * PASS:(b + 1) * PASS]
+            return load(name, block.rearrange("(p i) c -> p i c", i=PACK), F32, tag)
 
-        def page_rows(b, t):
-            return page0[b * PASS:(b + 1) * PASS, :].rearrange("(p t) c -> p t c", t=PACK)[:, t, :]
+        def load_page(b, t, tag=None):
+            rows = page0[b * PASS:(b + 1) * PASS, :].rearrange("(p t) c -> p t c", t=PACK)
+            page[b, t] = load(f"page{b}{t}", rows[:, t, :], F32, tag)
 
-        def load_gate(name, wg):
-            tile = kept(name, [P, S], F32)
-            nc.sync.dma_start(tile[:], wg)
-            return tile
+        def load_scale_rows(tile, rows, source_of):
+            for quad in range(QUADS):
+                nc.sync.dma_start(tile[QUAD * quad:QUAD * quad + rows, :].bitcast(I32),
+                                  source_of(slice(4 * quad, 4 * quad + 4)).bitcast(I32))
 
-
-        tab2_s = kept("tab2_s", [P, TM], U8)
-        w2_s = kept("w2_s", [P, H], U8)
-        tab_s = kept("tab_s", [P, T], U8)
-        w4_s = kept("w4_s", [P, 2, N], U8)
-
-        identity = kept("identity", [P, P], F32)
+        tab2_s = sbuf("tab2_s", [P, TM], U8)
+        w2_s = sbuf("w2_s", [P, H], U8)
+        tab_s = sbuf("tab_s", [P, T], U8)
+        w4_s = sbuf("w4_s", [P, 2 * N], U8)
+        identity = sbuf("identity", [P, P], F32)
         nc.gpsimd.memset(tab2_s[:].bitcast(I32), 0)
         make_identity(nc, identity[:])
         for tile in (w2_s, tab_s, w4_s):
             nc.gpsimd.memset(tile[:].bitcast(I32), 0)
 
-        w3_raw, w1_raw, w2_w, page = {}, {}, {}, {}
-
-        def load_w2(b):
-            w2_w[b] = kept(f"w2_w{b}", [P, PASS], I32)
-            nc.sync.dma_start(w2_w[b][:], words_of(w2_words, 0)[:, b * PASS:(b + 1) * PASS])
-
-        def load_page(b, t):
-            page[b, t] = load_big(f"page{b}{t}", page_rows(b, t), F32, PAGE_SLOT[b][t])
-
-        def load_scale_rows(tile, scales):
-            for quad in range(QUADS):
-                nc.sync.dma_start(tile[32 * quad:32 * quad + 4, :].bitcast(I32),
-                                  scales[0, 4 * quad:4 * quad + 4, :].bitcast(I32))
-
-        wg2_rows = load_gate("wg2_rows", wg2)
+        page, w1_raw, w2_w, w3_raw = {}, {}, {}, {}
+        wg2_rows = load("wg2_rows", wg2, F32)
         idx2 = load_list("idx2", offs2)
-        tab2_w = kept("tab2_w", [P, TM], I32)
-        nc.sync.dma_start(tab2_w[:], words_of(tab2_words, 0))
-        load_scale_rows(tab2_s, tab2_scales)
-        w3_raw[0] = load_big("w3_raw0", weight_block(w3, 0, 0), F32, 0)
-        load_w2(0)
-        load_scale_rows(w2_s, w2_scales)
+        tab2_w = load("tab2_w", words_of(tab2_words, 0), I32)
+        load_scale_rows(tab2_s, 4, lambda rows: tab2_scales[0, rows, :])
+        w3_raw[0] = load_weight("w3_raw0", w3, 0, 0, "w3_stage")
+        w2_w[0] = load("w2_w0", words_of(w2_words, 0)[:, :PASS], I32)
+        load_scale_rows(w2_s, 4, lambda rows: w2_scales[0, rows, :])
         idx4 = load_list("idx4", offs4)
         load_page(0, 0)
+        w2_w[1] = load("w2_w1", words_of(w2_words, 0)[:, PASS:], I32)
         load_page(0, 1)
         load_page(0, 2)
-        w3_raw[1] = load_big("w3_raw1", weight_block(w3, 0, 1), F32, 0)
-        load_w2(1)
+        w3_raw[1] = load_weight("w3_raw1", w3, 0, 1, "w3_stage")
         load_page(0, 3)
-        load_page(1, 0)
-        load_page(1, 1)
-        wg1_rows = load_gate("wg1_rows", wg1)
+        for t in range(LAST):
+            load_page(1, t)
+        wg1_rows = load("wg1_rows", wg1, F32)
         idx = load_list("idx", offs)
-        tab_w = [load_big("tab_w0", words_of(tab_words, 0), I32, 0)]
-        for quad in range(QUADS):
-            nc.sync.dma_start(tab_s[32 * quad:32 * quad + 8, :].bitcast(I32),
-                              tab_scales[:, 4 * quad:4 * quad + 4, :].bitcast(I32))
-        tab_w.append(load_big("tab_w1", words_of(tab_words, 1), I32, 4))
-        w1_raw[0, 0] = load_big("w1_raw00", weight_block(w1, 0, 0), F32, 6)
-        w1_raw[1, 0] = load_big("w1_raw10", weight_block(w1, 1, 0), F32, 7)
-        bias = kept("bias", [P, 2, PACK], F32)
-        gains = kept("gains", [P, 2, PACK], F32)
-        nc.sync.dma_start(bias[:], b1.rearrange("(b p t) -> p b t", b=2, t=PACK))
-        nc.sync.dma_start(gains[:], gain.rearrange("(b p t) -> p b t", b=2, t=PACK))
+        tab_w0 = load("tab_w0", words_of(tab_words, 0), I32, "w3_stage")
+        load_scale_rows(tab_s, 8, lambda rows: tab_scales[:, rows, :])
+        w1_raw[0, 0] = load_weight("w1_raw00", w1, 0, 0, "w1_stage0")
+        tab_w1 = load("tab_w1", words_of(tab_words, 1), I32)
+        w1_raw[1, 0] = load_weight("w1_raw10", w1, 1, 0, "w1_stage1")
+        bias = load("bias", b1.rearrange("(b p t) -> p b t", b=2, t=PACK), F32)
+        gains = load("gains", gain.rearrange("(b p t) -> p b t", b=2, t=PACK), F32)
         idx3 = load_list("idx3", offs3)
         idx5 = load_list("idx5", offs5)
-        w4_w = kept("w4_w", [P, 2, 2 * N], U8)
-        nc.sync.dma_start(w4_w[:].bitcast(I32), w4_words.rearrange("a p c -> p a c").bitcast(I32))
-        for quad in range(QUADS):
-            nc.sync.dma_start(w4_s[32 * quad:32 * quad + 4, :, :].bitcast(I32),
-                              w4_scales[:, 4 * quad:4 * quad + 4, :].rearrange("a r n -> r a n").bitcast(I32))
-        w1_raw[0, 1] = load_big("w1_raw01", weight_block(w1, 0, 1), F32, 6)
-        w1_raw[1, 1] = load_big("w1_raw11", weight_block(w1, 1, 1), F32, 7)
-        load_page(1, 2)
-        load_page(1, 3)
+        w4_w = load("w4_w", w4_words.rearrange("a p c -> p a c").bitcast(I32), I32)
+        load_scale_rows(w4_s, 4, lambda rows: w4_scales[:, rows, :].rearrange("a r n -> r a n"))
+        for a in range(2):
+            w1_raw[a, 1] = load_weight(f"w1_raw{a}1", w1, a, 1, f"w1_stage{a}")
+        load_page(1, LAST, "tab_w1")
 
-        def gather(out, window, offsets):
-            nc.vector.tensor_copy(out, window.indirect(offsets))
-
-        def round_weights(copy, raw, first, count, tag):
-            if tag is None:
-                rounded = ring.tile([P, count, P, PACK], BF16, name="rounded", tag="rounded", bufs=2, align_bytes=64)
-            else:
-                rounded = kept("rounded", [P, count, P, PACK], BF16, tag)
-            copy(rounded[:].rearrange("p (u e) q i -> p u q i e", e=2),
-                 raw[:].rearrange("p i (q u e) -> p u q i e", u=2, e=2)[:, first // 2:(first + count) // 2])
-            return rounded
+        def gather(name, window, offsets, count, tag=None, bufs=1):
+            picked = sbuf(name, [P, count], window.dtype, tag, bufs)
+            nc.vector.tensor_copy(picked[:], window.indirect(offsets))
+            return picked
 
         def quantise(codes, scales, rounded):
             nc.vector.quantize_mx(out=codes.bitcast(FP8X4), scales=scales, in_=rounded)
 
-        def round_shares(raw, shares, tag=None):
-            return [(round_weights(copy, raw, first, count, tag), first, count) for copy, first, count in shares]
+        def round_weight(copy, raw, first, count, tag="rounded", bufs=2):
+            rounded = sbuf("rounded", [P, count, P, PACK], BF16, tag, bufs)
+            copy(rounded[:].rearrange("p (u e) q i -> p u q i e", e=2),
+                 raw[:].rearrange("p i (q u e) -> p u q i e", u=2, e=2)[:, first // 2:(first + count) // 2])
+            return rounded, slice(first * P, (first + count) * P)
 
-        def quantise_weights(name, rounded, codes=None):
-            if codes is None:
-                codes = kept(name + "_codes", [P, PASS], U32)[:]
-            scales = kept(name + "_scales", [P, PASS], U8)
-            for tile, first, count in rounded:
-                cols = slice(first * P, (first + count) * P)
-                quantise(codes[:, cols], scales[:, cols], tile[:].rearrange("p t q i -> p (t q i)"))
+        def quantise_weight(name, parts, codes):
+            scales = sbuf(name + "_scales", [P, PASS], U8)
+            for rounded, cols in parts:
+                quantise(codes[:, cols], scales[:, cols], rounded[:].rearrange("p t q i -> p (t q i)"))
             return codes, scales
 
         def deal_w2(b):
-            codes = kept(f"w2_codes{b}", [P, PASS], I32)
-            scales = kept(f"w2_scales{b}", [P, PASS], U8)
+            codes = sbuf(f"w2_codes{b}", [P, PASS], I32)
+            scales = sbuf(f"w2_scales{b}", [P, PASS], U8)
             nc.vector.tensor_copy(codes[:].rearrange("p (u e q) -> p u q e", u=2, e=2),
                                   w2_w[b][:].rearrange("p (q u e) -> p u q e", u=2, e=2))
             nc.vector.tensor_copy(scales[:].rearrange("p (t q) -> p t q", t=PACK),
                                   w2_s[:, b * PASS:(b + 1) * PASS].rearrange("p (q t) -> p t q", t=PACK))
             return codes, scales
 
-        def bank(number, shape):
-            return psum.tile(shape, F32, name=f"bank{number}", tag=f"bank{number}")
-
-        def product(out, weights, t, moving, moving_scales, start, stop):
-            codes, scales = weights
+        def product(out, weight, t, moving, moving_scales, start, stop):
+            codes, scales = weight
             cols = slice(t * P, (t + 1) * P)
             nc.tensor.matmul_mx(out=out, lhsT=codes[:, cols].bitcast(FP8X4), lhsT_scale=scales[:, cols],
                                 rhs=moving.bitcast(FP8X4), rhs_scale=moving_scales, start=start, stop=stop)
 
         def turn_gate(rows):
-            turned = bank(6, [P, PACK, P])
+            turned = bank(6, [P, S // P, P])
             for c in range(S // P):
                 nc.tensor.transpose(turned[:, c, :], rows[:, c * P:(c + 1) * P], identity[:])
             return turned
 
         def deal_gate(name, turned, t):
-            columns = kept(f"columns{t % 2}", [P, S // P, QUADS, 32], F32)
+            columns = sbuf(f"columns{t % 2}", [P, S // P, QUADS, QUAD], F32)
             nc.scalar.copy(columns[:], turned[:].rearrange("p c (q t) -> p c t q", t=PACK)[:, :, t:t + 1, :]
-                           .to_broadcast([P, S // P, QUADS, 32]))
-            dealt = bank(7 if t % 2 == 0 else 0, [P, S])
+                           .to_broadcast([P, S // P, QUADS, QUAD]))
+            dealt = bank((7, 0)[t % 2], [P, S])
             for c in range(S // P):
-                nc.tensor.transpose(dealt[:, c * P:(c + 1) * P], columns[:, c].rearrange("p a q -> p (a q)"), identity[:])
-            gate = kept(f"{name}_{t}", [P, S], F32)
+                nc.tensor.transpose(dealt[:, c * P:(c + 1) * P], columns[:, c].rearrange("p a q -> p (a q)"),
+                                    identity[:])
+            gate = sbuf(f"{name}_{t}", [P, S], F32)
             nc.scalar.copy(gate[:], dealt[:])
-            return gate[:]
+            return gate
 
-        v2_w = kept("v2_w", [P, S], U32)
-        v2_s = kept("v2_s", [P, S], U8)
-        gather(v2_w[:], tab2_w[:].bitcast(U32), idx2[:])
-        gather(v2_s[:], tab2_s[:], idx2[:])
+        e2, e3, h1, h2 = {}, {}, {}, {}
 
-        h1, h2, e23 = {}, {}, {}
-
-        def soil_features(b, w2_q, w3_q):
+        def soil_products(b, w2_q, w3_q):
             for t in range(PACK):
                 e3_bank = bank(t % 2, [P, S])
                 product(e3_bank[:], w3_q, t, v2_w[:], v2_s[:], True, True)
-                e2_bank = bank(2 + t, [P, S])
-                product(e2_bank[:], w2_q, t, v2_w[:], v2_s[:], True, True)
+                e2[b, t] = bank(2 + t, [P, S])
+                product(e2[b, t][:], w2_q, t, v2_w[:], v2_s[:], True, True)
                 if b == 0 and t < 2:
-                    e3 = kept("e3", [P, S], F32, f"columns{1 - t}")
+                    e3[b, t] = sbuf("e3", [P, S], F32, f"columns{1 - t}")
                 else:
-                    e3 = ring.tile([P, S], F32, name="e3", tag="e3", bufs=4)
-                nc.scalar.copy(e3[:], e3_bank[:])
-                e23[b, t] = (e2_bank, e3)
+                    e3[b, t] = sbuf("e3", [P, S], F32, bufs=PACK)
+                nc.scalar.copy(e3[b, t][:], e3_bank[:])
 
-        def larger(b, t):
-            if b == 0 or t < 2:
-                h2[b, t] = kept("h2", [P, S], F32, bufs=2)
-            else:
-                h2[b, t] = kept(f"h2_1{t}", [P, S], F32, "x_bf00")
-            nc.vector.tensor_tensor(h2[b, t][:], e23[b, t][0][:], e23[b, t][1][:], ALU.max)
+        def soil_maximum(b, t, tag="h2", bufs=2):
+            h2[b, t] = sbuf("h2", [P, S], F32, tag, bufs)
+            nc.vector.tensor_tensor(h2[b, t][:], e2[b, t][:], e3[b, t][:], ALU.max)
 
-        def cutter_features(b, w1_q):
+        def cutter_products(b, w1_q):
             for t in range(PACK):
                 acc = bank(6 + t % 2, [P, S])
                 for a in range(2):
                     product(acc[:], w1_q[a], t, v_w[a][:], v_s[4 * a:P, :], a == 0, a == 1)
-                h1[b, t] = kept(f"h1_{b}{t}", [P, S], F32)
+                h1[b, t] = sbuf(f"h1_{b}{t}", [P, S], F32)
                 nc.scalar.activation(h1[b, t][:], acc[:], ACT.Identity, bias=bias[:, b, t:t + 1])
 
         def put(b, t, offsets, values, gate):
-            nc.vector.tensor_tensor(page[b, t][:].indirect(offsets[:]), values[:], gate[t], ALU.mult)
+            nc.vector.tensor_tensor(page[b, t][:].indirect(offsets[:]), values[b, t][:], gate[t][:], ALU.mult)
 
-        x_bf = [[kept(f"x_bf0{c}", [P, R // 2, PACK], BF16) for c in range(2)],
-                [kept(f"x_bf1{c}", [P, CHUNK, PACK], BF16) for c in range(R // CHUNK)]]
-        x_codes, x_scales = {}, {}
+        x_width = [R // 2, CHUNK]
+        x_bf = {(b, first): sbuf(f"x_bf{b}_{first}", [P, x_width[b], PACK], BF16)
+                for b in range(2) for first in range(0, R, x_width[b])}
+        x_q = {}
 
-        def read_slots(b, t, first, count):
-            if count == R:
-                picked = kept(f"picked{b}{t}", [P, R], F32, PICKED_TAG[b][t])
-            else:
-                picked = ring.tile([P, count], F32, name="picked", tag=f"picked{count}", bufs=2)
-            gather(picked[:], page[b, t][:], idx5[:, first // 16:(first + count) // 16])
-            if count == R:
-                squashed = keep.tile([P, R], F32, name="squashed", tag="slot7", align_bytes=64)[:]
-            else:
-                c = first // CHUNK
-                if c in HELD:
-                    squashed = kept(f"squashed{c}", [P, count], F32, f"x_codes1{HELD[c] * CHUNK}")[:]
-                else:
-                    squashed = last_squashed[:, first:first + count]
-            nc.scalar.activation(squashed, picked[:], ACT.Tanh)
-            width = R // len(x_bf[b])
-            for j in range(0, count, width):
-                plane = x_bf[b][(first + j) // width][:, :, t]
-                if count == R:
-                    nc.scalar.activation(plane, squashed[:, j:j + width], ACT.Copy, scale=gains[:, b, t:t + 1])
-                else:
-                    nc.vector.tensor_scalar(plane, squashed[:, j:j + width], gains[:, b, t:t + 1], None, ALU.mult)
+        def gain_on_scalar(b, t, first, squashed):
+            nc.scalar.activation(x_bf[b, first][:, :, t], squashed[:, first:first + x_width[b]], ACT.Copy,
+                                 scale=gains[:, b, t:t + 1])
 
-        def quantise_x(b, first, count):
-            codes = kept(f"x_codes{b}{first}", [P, count], U32)
-            rounded = x_bf[b][first // count][:]
-            scales = kept(f"x_scales{b}{first}", [P, count], U8)
-            quantise(codes[:], scales[:], rounded.rearrange("p j t -> p (j t)"))
-            for j in range(0, count, YCOLS):
-                x_codes[b, (first + j) // YCOLS] = codes[:, j:j + YCOLS]
-                x_scales[b, (first + j) // YCOLS] = scales[:, j:j + YCOLS]
+        def gain_on_vector(b, t, first, squashed):
+            nc.vector.tensor_scalar(x_bf[b, first][:, :, t], squashed[:, first:first + x_width[b]],
+                                    gains[:, b, t:t + 1], None, ALU.mult)
 
+        def squashed_tile():
+            return sbuf("squashed", [P, R], F32, "w1_stage1")
+
+        def read_slots(b, t, tag):
+            picked = gather("picked", page[b, t][:], idx5[:], R, tag)
+            squashed = squashed_tile()
+            nc.scalar.activation(squashed[:], picked[:], ACT.Tanh)
+            for first in range(0, R, x_width[b]):
+                gain_on_scalar(b, t, first, squashed)
+
+        def quantise_x(b, first):
+            codes = sbuf(f"x_codes{b}_{first}", [P, x_width[b]], U32)
+            scales = sbuf(f"x_scales{b}_{first}", [P, x_width[b]], U8)
+            quantise(codes[:], scales[:], x_bf[b, first][:].rearrange("p j t -> p (j t)"))
+            for j in range(0, x_width[b], BANK_SLOTS):
+                x_q[b, (first + j) // BANK_SLOTS] = codes[:, j:j + BANK_SLOTS], scales[:, j:j + BANK_SLOTS]
+
+        def new_codes(name):
+            return sbuf(name, [P, PASS], U32)
+
+        v2_w = gather("v2_w", tab2_w[:].bitcast(U32), idx2[:], S)
+        v2_s = gather("v2_s", tab2_s[:], idx2[:], S)
         turned = turn_gate(wg2_rows)
         gate2 = [deal_gate("gate2", turned, 0)]
-        w3_q = quantise_weights("w3_0", round_shares(w3_raw[0], [(nc.vector.tensor_copy, 0, 2), (nc.scalar.copy, 2, 2)]))
-        soil_features(0, deal_w2(0), w3_q)
+        w3_parts = [round_weight(nc.vector.tensor_copy, w3_raw[0], 0, 2), round_weight(nc.scalar.copy, w3_raw[0], 2, 2)]
+        w3_q = quantise_weight("w3_0", w3_parts, new_codes("w3_0_codes"))
+        soil_products(0, deal_w2(0), w3_q)
         gate2.extend(deal_gate("gate2", turned, t) for t in range(1, PACK))
-        larger(0, 0)
-        larger(0, 1)
-        put(0, 0, idx4, h2[0, 0], gate2)
-        larger(0, 2)
-
-        put(0, 1, idx4, h2[0, 1], gate2)
-        larger(0, 3)
-        put(0, 2, idx4, h2[0, 2], gate2)
-        whole = [(nc.scalar.copy, 0, PACK)]
-        soil_features(1, deal_w2(1), quantise_weights("w3_1", round_shares(w3_raw[1], whole)))
-        put(0, 3, idx4, h2[0, 3], gate2)
-        for t in range(2):
-            larger(1, t)
-            put(1, t, idx4, h2[1, t], gate2)
+        soil_maximum(0, 0)
+        for t in range(LAST):
+            soil_maximum(0, t + 1)
+            put(0, t, idx4, h2, gate2)
+        w2_q = deal_w2(1)
+        w3_parts = [round_weight(nc.scalar.copy, w3_raw[1], 0, PACK)]
+        soil_products(1, w2_q, quantise_weight("w3_1", w3_parts, new_codes("w3_1_codes")))
+        put(0, LAST, idx4, h2, gate2)
+        for t in range(LAST):
+            soil_maximum(1, t)
+            put(1, t, idx4, h2, gate2)
 
         turned = turn_gate(wg1_rows)
         gate1 = [deal_gate("gate1", turned, t) for t in range(PACK)]
-        v_w = [kept(f"v_w{a}", [P, S], U32) for a in range(2)]
-        v_s = kept("v_s", [P, S], U8)
-        gather(v_w[0][:], tab_w[0][:].bitcast(U32), idx[:])
-        gather(v_s[:], tab_s[:], idx[:])
-        gather(v_w[1][:], tab_w[1][:].bitcast(U32), idx[:])
-        cutter_features(0, [quantise_weights(f"w1_{a}0", round_shares(w1_raw[a, 0], whole, [None, "w4_codes"][a])) for a in range(2)])
-        w4_codes = kept("w4_codes", [P, 2 * 2 * N], U8)
-        w4_sc = kept("w4_sc", [P, 2 * N], U8)
-        nc.vector.tensor_copy(w4_codes[:].bitcast(U16).rearrange("p (a t q) -> p a t q", a=2, t=PACK),
+        v_w = [gather("v_w0", tab_w0[:].bitcast(U32), idx[:], S)]
+        v_s = gather("v_s", tab_s[:], idx[:], S)
+        v_w.append(gather("v_w1", tab_w1[:].bitcast(U32), idx[:], S))
+        w1_q = [quantise_weight("w1_00", [round_weight(nc.scalar.copy, w1_raw[0, 0], 0, PACK)], new_codes("w1_00_codes"))]
+        w1_parts = [round_weight(nc.scalar.copy, w1_raw[1, 0], first, 2, tag, 1)
+                    for first, tag in ((0, "w4_codes"), (2, "w4_dealt_scales"))]
+        w1_q.append(quantise_weight("w1_10", w1_parts, new_codes("w1_10_codes")))
+        cutter_products(0, w1_q)
+        w4_codes = sbuf("w4_codes", [P, 2 * N], U16)
+        w4_dealt_scales = sbuf("w4_dealt_scales", [P, 2 * N], U8)
+        nc.vector.tensor_copy(w4_codes[:].rearrange("p (a t q) -> p a t q", a=2, t=PACK),
                               w4_w[:].bitcast(U16).rearrange("p a (q t) -> p a t q", t=PACK))
-        nc.vector.tensor_copy(w4_sc[:].rearrange("p (a t q) -> p a t q", a=2, t=PACK),
-                              w4_s[:].rearrange("p a (q t) -> p a t q", t=PACK))
+        nc.vector.tensor_copy(w4_dealt_scales[:].rearrange("p (a t q) -> p a t q", a=2, t=PACK),
+                              w4_s[:].rearrange("p (a q t) -> p a t q", a=2, t=PACK))
 
-        w1_bf = [round_shares(w1_raw[a, 1], whole) for a in range(2)]
+        w1_parts = [[round_weight(nc.scalar.copy, w1_raw[a, 1], 0, PACK)] for a in range(2)]
         for t in range(PACK):
-            put(0, t, idx3, h1[0, t], gate1)
+            put(0, t, idx3, h1, gate1)
             if t == 2:
-                late_codes = kept("late_codes", [P, 2, PASS], U32, "slot5")
-                cutter_features(1, [quantise_weights(f"w1_{a}1", w1_bf[a], late_codes[:, a, :]) for a in range(2)])
-            read_slots(0, t, 0, R)
+                late_codes = sbuf("late_codes", [P, 2, PASS], U32, "page02")
+                cutter_products(1, [quantise_weight(f"w1_{a}1", w1_parts[a], late_codes[:, a, :]) for a in range(2)])
+            read_slots(0, t, "picked_a" if t == 0 else "picked_b")
 
-        for t in range(PACK):
-            if t >= 2:
-                put(1, t, idx4, h2[1, t], gate2)
-            put(1, t, idx3, h1[1, t], gate1)
-            if t == 1:
-                quantise_x(0, 0, R // 2)
-                quantise_x(0, R // 2, R // 2)
-            if t in (1, 2):
-                larger(1, t + 1)
-            if t < PACK - 1:
-                read_slots(1, t, 0, R)
+        put(1, 0, idx3, h1, gate1)
+        read_slots(1, 0, "picked_a")
+        put(1, 1, idx3, h1, gate1)
+        read_slots(1, 1, "picked_b")
+        put(1, 2, idx3, h1, gate1)
+        quantise_x(0, 0)
+        quantise_x(0, R // 2)
+        soil_maximum(1, LAST, "x_bf0_0", 1)
+        read_slots(1, 2, f"x_bf0_{R // 2}")
+        put(1, LAST, idx4, h2, gate2)
+        put(1, LAST, idx3, h1, gate1)
 
-        def last_product(acc, c, a):
+        def last_product(c, a):
+            codes, scales = x_q[a, c]
             for t in range(PACK):
-                n0 = (a * PACK + t) * P
-                nc.tensor.matmul_mx(out=acc[:, t, :], lhsT=w4_codes[:, 2 * n0:2 * n0 + 2 * P].bitcast(FP4X4),
-                                    lhsT_scale=w4_sc[:, n0:n0 + P],
-                                    rhs=x_codes[a, c].bitcast(FP8X4), rhs_scale=x_scales[a, c],
-                                    start=(a == 0 and t == 0), stop=(a == 1 and t == PACK - 1))
+                cols = slice((a * PACK + t) * P, (a * PACK + t + 1) * P)
+                nc.tensor.matmul_mx(out=y_banks[c][:, t, :], lhsT=w4_codes[:, cols].bitcast(FP4X4),
+                                    lhsT_scale=w4_dealt_scales[:, cols], rhs=codes.bitcast(FP8X4), rhs_scale=scales,
+                                    start=(a == 0 and t == 0), stop=(a == 1 and t == LAST))
 
-        y_banks = [bank(Y_BANK[c], [P, PACK, YCOLS]) for c in range(R // YCOLS)]
-        for c in range(R // YCOLS):
-            last_product(y_banks[c], c, 0)
+        y_banks = [bank(c, [P, PACK, BANK_SLOTS]) for c in range(R // BANK_SLOTS)]
+        for c in range(R // BANK_SLOTS):
+            last_product(c, 0)
 
-        last_squashed = keep.tile([P, R], F32, name="squashed", tag="slot7", align_bytes=64)
-        y_codes = kept("y_codes", [P, R], U32)
-        y_scales = kept("y_scales", [P, R], U8)
+        squashed = squashed_tile()
+        y_codes = sbuf("y_codes", [P, R], U32)
+        y_scales = sbuf("y_scales", [P, R], U8)
         y_rows = out_0.rearrange("(p t) j -> p t j", t=PACK)
         y_words = words_of(out_1, 0)
-        for first in range(0, R, CHUNK):
+        for chunk in range(R // CHUNK):
+            first = chunk * CHUNK
             cols = slice(first, first + CHUNK)
-            read_slots(1, PACK - 1, first, CHUNK)
-            quantise_x(1, first, CHUNK)
-            y = keep.tile([P, PACK, CHUNK], F32, name="y", tag=f"slot{Y_SLOT[first // CHUNK]}", align_bytes=64)
-            y_bf = ring.tile([P, CHUNK, PACK], BF16, name="y_bf", tag="rounded", bufs=2, align_bytes=64)
-            for part in range(CHUNK // YCOLS):
-                c = first // YCOLS + part
-                last_product(y_banks[c], c, 1)
-                copy = nc.vector.tensor_copy if c in VECTOR_BANKS else nc.scalar.copy
-                copy(y[:, :, part * YCOLS:(part + 1) * YCOLS], y_banks[c][:])
-                nc.vector.tensor_copy(
-                    y_bf[:, part * YCOLS:(part + 1) * YCOLS, :].rearrange("p (c i) t -> p c t i", i=2),
-                    y[:, :, part * YCOLS:(part + 1) * YCOLS].rearrange("p t (c i) -> p c t i", i=2))
+            picked = gather("picked_chunk", page[1, LAST][:],
+                            idx5[:, first // LIST_ROWS:(first + CHUNK) // LIST_ROWS], CHUNK, bufs=2)
+            nc.scalar.activation(squashed[:, cols], picked[:], ACT.Tanh)
+            apply_gain = gain_on_scalar if chunk == SCALAR_GAIN_CHUNK else gain_on_vector
+            apply_gain(1, LAST, first, squashed)
+            quantise_x(1, first)
+            y = sbuf("y", [P, PACK, CHUNK], F32, f"page0{chunk}")
+            y_bf = sbuf("y_bf", [P, CHUNK, PACK], BF16, "rounded", 2)
+            for j in range(0, CHUNK, BANK_SLOTS):
+                c = (first + j) // BANK_SLOTS
+                last_product(c, 1)
+                nc.scalar.copy(y[:, :, j:j + BANK_SLOTS], y_banks[c][:])
+                nc.vector.tensor_copy(y_bf[:, j:j + BANK_SLOTS, :].rearrange("p (s e) t -> p s t e", e=2),
+                                      y[:, :, j:j + BANK_SLOTS].rearrange("p t (s e) -> p s t e", e=2))
             nc.sync.dma_start(y_rows[:, :, cols], y[:])
             quantise(y_codes[:, cols], y_scales[:, cols], y_bf[:].rearrange("p j t -> p (j t)"))
-            if first + CHUNK in WORD_STORES:
-                done = slice(WORD_STORES[first + CHUNK], first + CHUNK)
-                nc.sync.dma_start(y_words[:, done], y_codes[:, done].bitcast(I32))
+            if chunk % 2 == 1:
+                pair = slice(first - CHUNK, first + CHUNK)
+                nc.sync.dma_start(y_words[:, pair], y_codes[:, pair].bitcast(I32))
         for quad in range(QUADS):
             queue = nc.scalar if quad % 2 else nc.sync
             queue.dma_start(out_2[0, 4 * quad:4 * quad + 4, :].bitcast(I32),
-                            y_scales[32 * quad:32 * quad + 4, :].bitcast(I32))
+                            y_scales[QUAD * quad:QUAD * quad + 4, :].bitcast(I32))

from contextlib import ExitStack

import concourse.mybir as mybir
from concourse.masks import make_identity

K, M, H, N, T, TM, S, R = 1024, 512, 1024, 512, 2048, 1024, 512, 1024
FLOPS = 2 * (K * H * S + 2 * M * H * S + H * N * R)

F32 = mybir.dt.float32
BF16 = mybir.dt.bfloat16
I32 = mybir.dt.int32
U32 = mybir.dt.uint32
U16 = mybir.dt.uint16
U8 = mybir.dt.uint8
FP8X4 = mybir.dt.float8_e4m3fn_x4
FP4X4 = mybir.dt.float4_e2m1fn_x4
ALU = mybir.AluOpType
ACT = mybir.ActivationFunctionType

P = 128
PACK = 4
PASS = P * PACK
QUAD = 32
QUADS = P // QUAD
LIST_ROWS = 16
LAST = PACK - 1
CHUNK = 256
BANK_SLOTS = 128
SCALAR_GAIN_CHUNK = 1


def tile_list_ring_advance_features_kernel(
    tc, tab_words, tab_scales, tab2_words, tab2_scales, offs, offs2, offs3, offs4, offs5,
    w1, b1, w2_words, w2_scales, w3, wg1, wg2, page0, gain, w4_words, w4_scales,
    out_0, out_1, out_2,
):
    nc = tc.nc
    with ExitStack() as ctx:
        lists = ctx.enter_context(tc.tile_pool(name="lists", bufs=1))
        keep = ctx.enter_context(tc.tile_pool(name="keep", bufs=1))
        psum = ctx.enter_context(tc.psum_pool(name="psum", bufs=1))

        def sbuf(name, shape, dtype, tag=None, bufs=1):
            return keep.tile(shape, dtype, name=name, tag=tag or name, bufs=bufs, align_bytes=64)

        def bank(number, shape):
            return psum.tile(shape, F32, name=f"bank{number}", tag=f"bank{number}")

        def load(name, source, dtype, tag=None):
            tile = sbuf(name, list(source.shape), dtype, tag)
            nc.sync.dma_start(tile[:], source)
            return tile

        def load_list(name, source):
            tile = lists.tile(list(source.shape), U16, name=name)
            nc.sync.dma_start(tile[:], source)
            return tile

        def words_of(words, a):
            return words[a].rearrange("p c i -> p (c i)").bitcast(I32)

        def load_weight(name, w, a, b, tag):
            block = w[a * PASS:(a + 1) * PASS, b * PASS:(b + 1) * PASS]
            return load(name, block.rearrange("(p i) c -> p i c", i=PACK), F32, tag)

        def load_page(b, t, tag=None):
            rows = page0[b * PASS:(b + 1) * PASS, :].rearrange("(p t) c -> p t c", t=PACK)
            page[b, t] = load(f"page{b}{t}", rows[:, t, :], F32, tag)

        def load_scale_rows(tile, rows, source_of):
            for quad in range(QUADS):
                nc.sync.dma_start(tile[QUAD * quad:QUAD * quad + rows, :].bitcast(I32),
                                  source_of(slice(4 * quad, 4 * quad + 4)).bitcast(I32))

        tab2_s = sbuf("tab2_s", [P, TM], U8)
        w2_s = sbuf("w2_s", [P, H], U8)
        tab_s = sbuf("tab_s", [P, T], U8)
        w4_s = sbuf("w4_s", [P, 2 * N], U8)
        identity = sbuf("identity", [P, P], F32)
        nc.gpsimd.memset(tab2_s[:].bitcast(I32), 0)
        make_identity(nc, identity[:])
        for tile in (w2_s, tab_s, w4_s):
            nc.gpsimd.memset(tile[:].bitcast(I32), 0)

        page, w1_raw, w2_w, w3_raw = {}, {}, {}, {}
        wg2_rows = load("wg2_rows", wg2, F32)
        idx2 = load_list("idx2", offs2)
        tab2_w = load("tab2_w", words_of(tab2_words, 0), I32)
        load_scale_rows(tab2_s, 4, lambda rows: tab2_scales[0, rows, :])
        w3_raw[0] = load_weight("w3_raw0", w3, 0, 0, "w3_stage")
        w2_w[0] = load("w2_w0", words_of(w2_words, 0)[:, :PASS], I32)
        load_scale_rows(w2_s, 4, lambda rows: w2_scales[0, rows, :])
        idx4 = load_list("idx4", offs4)
        load_page(0, 0)
        w2_w[1] = load("w2_w1", words_of(w2_words, 0)[:, PASS:], I32)
        load_page(0, 1)
        load_page(0, 2)
        w3_raw[1] = load_weight("w3_raw1", w3, 0, 1, "w3_stage")
        load_page(0, 3)
        for t in range(LAST):
            load_page(1, t)
        wg1_rows = load("wg1_rows", wg1, F32)
        idx = load_list("idx", offs)
        tab_w0 = load("tab_w0", words_of(tab_words, 0), I32, "w3_stage")
        load_scale_rows(tab_s, 8, lambda rows: tab_scales[:, rows, :])
        w1_raw[0, 0] = load_weight("w1_raw00", w1, 0, 0, "w1_stage0")
        tab_w1 = load("tab_w1", words_of(tab_words, 1), I32)
        w1_raw[1, 0] = load_weight("w1_raw10", w1, 1, 0, "w1_stage1")
        bias = load("bias", b1.rearrange("(b p t) -> p b t", b=2, t=PACK), F32)
        gains = load("gains", gain.rearrange("(b p t) -> p b t", b=2, t=PACK), F32)
        idx3 = load_list("idx3", offs3)
        idx5 = load_list("idx5", offs5)
        w4_w = load("w4_w", w4_words.rearrange("a p c -> p a c").bitcast(I32), I32)
        load_scale_rows(w4_s, 4, lambda rows: w4_scales[:, rows, :].rearrange("a r n -> r a n"))
        for a in range(2):
            w1_raw[a, 1] = load_weight(f"w1_raw{a}1", w1, a, 1, f"w1_stage{a}")
        load_page(1, LAST, "tab_w1")

        def gather(name, window, offsets, count, tag=None, bufs=1):
            picked = sbuf(name, [P, count], window.dtype, tag, bufs)
            nc.vector.tensor_copy(picked[:], window.indirect(offsets))
            return picked

        def quantise(codes, scales, rounded):
            nc.vector.quantize_mx(out=codes.bitcast(FP8X4), scales=scales, in_=rounded)

        def round_weight(copy, raw, first, count, tag="rounded", bufs=2):
            rounded = sbuf("rounded", [P, count, P, PACK], BF16, tag, bufs)
            copy(rounded[:].rearrange("p (u e) q i -> p u q i e", e=2),
                 raw[:].rearrange("p i (q u e) -> p u q i e", u=2, e=2)[:, first // 2:(first + count) // 2])
            return rounded, slice(first * P, (first + count) * P)

        def quantise_weight(name, parts, codes):
            scales = sbuf(name + "_scales", [P, PASS], U8)
            for rounded, cols in parts:
                quantise(codes[:, cols], scales[:, cols], rounded[:].rearrange("p t q i -> p (t q i)"))
            return codes, scales

        def deal_w2(b):
            codes = sbuf(f"w2_codes{b}", [P, PASS], I32)
            scales = sbuf(f"w2_scales{b}", [P, PASS], U8)
            nc.vector.tensor_copy(codes[:].rearrange("p (u e q) -> p u q e", u=2, e=2),
                                  w2_w[b][:].rearrange("p (q u e) -> p u q e", u=2, e=2))
            nc.vector.tensor_copy(scales[:].rearrange("p (t q) -> p t q", t=PACK),
                                  w2_s[:, b * PASS:(b + 1) * PASS].rearrange("p (q t) -> p t q", t=PACK))
            return codes, scales

        def product(out, weight, t, moving, moving_scales, start, stop):
            codes, scales = weight
            cols = slice(t * P, (t + 1) * P)
            nc.tensor.matmul_mx(out=out, lhsT=codes[:, cols].bitcast(FP8X4), lhsT_scale=scales[:, cols],
                                rhs=moving.bitcast(FP8X4), rhs_scale=moving_scales, start=start, stop=stop)

        def turn_gate(rows):
            turned = bank(6, [P, S // P, P])
            for c in range(S // P):
                nc.tensor.transpose(turned[:, c, :], rows[:, c * P:(c + 1) * P], identity[:])
            return turned

        def deal_gate(name, turned, t):
            columns = sbuf(f"columns{t % 2}", [P, S // P, QUADS, QUAD], F32)
            nc.scalar.copy(columns[:], turned[:].rearrange("p c (q t) -> p c t q", t=PACK)[:, :, t:t + 1, :]
                           .to_broadcast([P, S // P, QUADS, QUAD]))
            dealt = bank((7, 0)[t % 2], [P, S])
            for c in range(S // P):
                nc.tensor.transpose(dealt[:, c * P:(c + 1) * P], columns[:, c].rearrange("p a q -> p (a q)"),
                                    identity[:])
            gate = sbuf(f"{name}_{t}", [P, S], F32)
            nc.scalar.copy(gate[:], dealt[:])
            return gate

        e2, e3, h1, h2 = {}, {}, {}, {}

        def soil_products(b, w2_q, w3_q):
            for t in range(PACK):
                e3_bank = bank(t % 2, [P, S])
                product(e3_bank[:], w3_q, t, v2_w[:], v2_s[:], True, True)
                e2[b, t] = bank(2 + t, [P, S])
                product(e2[b, t][:], w2_q, t, v2_w[:], v2_s[:], True, True)
                if b == 0 and t < 2:
                    e3[b, t] = sbuf("e3", [P, S], F32, f"columns{1 - t}")
                else:
                    e3[b, t] = sbuf("e3", [P, S], F32, bufs=PACK)
                nc.scalar.copy(e3[b, t][:], e3_bank[:])

        def soil_maximum(b, t, tag="h2", bufs=2):
            h2[b, t] = sbuf("h2", [P, S], F32, tag, bufs)
            nc.vector.tensor_tensor(h2[b, t][:], e2[b, t][:], e3[b, t][:], ALU.max)

        def cutter_products(b, w1_q):
            for t in range(PACK):
                acc = bank(6 + t % 2, [P, S])
                for a in range(2):
                    product(acc[:], w1_q[a], t, v_w[a][:], v_s[4 * a:P, :], a == 0, a == 1)
                h1[b, t] = sbuf(f"h1_{b}{t}", [P, S], F32)
                nc.scalar.activation(h1[b, t][:], acc[:], ACT.Identity, bias=bias[:, b, t:t + 1])

        def put(b, t, offsets, values, gate):
            nc.vector.tensor_tensor(page[b, t][:].indirect(offsets[:]), values[b, t][:], gate[t][:], ALU.mult)

        x_width = [R // 2, CHUNK]
        x_bf = {(b, first): sbuf(f"x_bf{b}_{first}", [P, x_width[b], PACK], BF16)
                for b in range(2) for first in range(0, R, x_width[b])}
        x_q = {}

        def gain_on_scalar(b, t, first, squashed):
            nc.scalar.activation(x_bf[b, first][:, :, t], squashed[:, first:first + x_width[b]], ACT.Copy,
                                 scale=gains[:, b, t:t + 1])

        def gain_on_vector(b, t, first, squashed):
            nc.vector.tensor_scalar(x_bf[b, first][:, :, t], squashed[:, first:first + x_width[b]],
                                    gains[:, b, t:t + 1], None, ALU.mult)

        def squashed_tile():
            return sbuf("squashed", [P, R], F32, "w1_stage1")

        def read_slots(b, t, tag):
            picked = gather("picked", page[b, t][:], idx5[:], R, tag)
            squashed = squashed_tile()
            nc.scalar.activation(squashed[:], picked[:], ACT.Tanh)
            for first in range(0, R, x_width[b]):
                gain_on_scalar(b, t, first, squashed)

        def quantise_x(b, first):
            codes = sbuf(f"x_codes{b}_{first}", [P, x_width[b]], U32)
            scales = sbuf(f"x_scales{b}_{first}", [P, x_width[b]], U8)
            quantise(codes[:], scales[:], x_bf[b, first][:].rearrange("p j t -> p (j t)"))
            for j in range(0, x_width[b], BANK_SLOTS):
                x_q[b, (first + j) // BANK_SLOTS] = codes[:, j:j + BANK_SLOTS], scales[:, j:j + BANK_SLOTS]

        def new_codes(name):
            return sbuf(name, [P, PASS], U32)

        v2_w = gather("v2_w", tab2_w[:].bitcast(U32), idx2[:], S)
        v2_s = gather("v2_s", tab2_s[:], idx2[:], S)
        turned = turn_gate(wg2_rows)
        gate2 = [deal_gate("gate2", turned, 0)]
        w3_parts = [round_weight(nc.vector.tensor_copy, w3_raw[0], 0, 2), round_weight(nc.scalar.copy, w3_raw[0], 2, 2)]
        w3_q = quantise_weight("w3_0", w3_parts, new_codes("w3_0_codes"))
        soil_products(0, deal_w2(0), w3_q)
        gate2.extend(deal_gate("gate2", turned, t) for t in range(1, PACK))
        soil_maximum(0, 0)
        for t in range(LAST):
            soil_maximum(0, t + 1)
            put(0, t, idx4, h2, gate2)
        w2_q = deal_w2(1)
        w3_parts = [round_weight(nc.scalar.copy, w3_raw[1], 0, PACK)]
        soil_products(1, w2_q, quantise_weight("w3_1", w3_parts, new_codes("w3_1_codes")))
        put(0, LAST, idx4, h2, gate2)
        for t in range(LAST):
            soil_maximum(1, t)
            put(1, t, idx4, h2, gate2)

        turned = turn_gate(wg1_rows)
        gate1 = [deal_gate("gate1", turned, t) for t in range(PACK)]
        v_w = [gather("v_w0", tab_w0[:].bitcast(U32), idx[:], S)]
        v_s = gather("v_s", tab_s[:], idx[:], S)
        v_w.append(gather("v_w1", tab_w1[:].bitcast(U32), idx[:], S))
        w1_q = [quantise_weight("w1_00", [round_weight(nc.scalar.copy, w1_raw[0, 0], 0, PACK)], new_codes("w1_00_codes"))]
        w1_parts = [round_weight(nc.scalar.copy, w1_raw[1, 0], first, 2, tag, 1)
                    for first, tag in ((0, "w4_codes"), (2, "w4_dealt_scales"))]
        w1_q.append(quantise_weight("w1_10", w1_parts, new_codes("w1_10_codes")))
        cutter_products(0, w1_q)
        w4_codes = sbuf("w4_codes", [P, 2 * N], U16)
        w4_dealt_scales = sbuf("w4_dealt_scales", [P, 2 * N], U8)
        nc.vector.tensor_copy(w4_codes[:].rearrange("p (a t q) -> p a t q", a=2, t=PACK),
                              w4_w[:].bitcast(U16).rearrange("p a (q t) -> p a t q", t=PACK))
        nc.vector.tensor_copy(w4_dealt_scales[:].rearrange("p (a t q) -> p a t q", a=2, t=PACK),
                              w4_s[:].rearrange("p (a q t) -> p a t q", a=2, t=PACK))

        w1_parts = [[round_weight(nc.scalar.copy, w1_raw[a, 1], 0, PACK)] for a in range(2)]
        for t in range(PACK):
            put(0, t, idx3, h1, gate1)
            if t == 2:
                late_codes = sbuf("late_codes", [P, 2, PASS], U32, "page02")
                cutter_products(1, [quantise_weight(f"w1_{a}1", w1_parts[a], late_codes[:, a, :]) for a in range(2)])
            read_slots(0, t, "picked_a" if t == 0 else "picked_b")

        put(1, 0, idx3, h1, gate1)
        read_slots(1, 0, "picked_a")
        put(1, 1, idx3, h1, gate1)
        read_slots(1, 1, "picked_b")
        put(1, 2, idx3, h1, gate1)
        quantise_x(0, 0)
        quantise_x(0, R // 2)
        soil_maximum(1, LAST, "x_bf0_0", 1)
        read_slots(1, 2, f"x_bf0_{R // 2}")
        put(1, LAST, idx4, h2, gate2)
        put(1, LAST, idx3, h1, gate1)

        def last_product(c, a):
            codes, scales = x_q[a, c]
            for t in range(PACK):
                cols = slice((a * PACK + t) * P, (a * PACK + t + 1) * P)
                nc.tensor.matmul_mx(out=y_banks[c][:, t, :], lhsT=w4_codes[:, cols].bitcast(FP4X4),
                                    lhsT_scale=w4_dealt_scales[:, cols], rhs=codes.bitcast(FP8X4), rhs_scale=scales,
                                    start=(a == 0 and t == 0), stop=(a == 1 and t == LAST))

        y_banks = [bank(c, [P, PACK, BANK_SLOTS]) for c in range(R // BANK_SLOTS)]
        for c in range(R // BANK_SLOTS):
            last_product(c, 0)

        squashed = squashed_tile()
        y_codes = sbuf("y_codes", [P, R], U32)
        y_scales = sbuf("y_scales", [P, R], U8)
        y_rows = out_0.rearrange("(p t) j -> p t j", t=PACK)
        y_words = words_of(out_1, 0)
        for chunk in range(R // CHUNK):
            first = chunk * CHUNK
            cols = slice(first, first + CHUNK)
            picked = gather("picked_chunk", page[1, LAST][:],
                            idx5[:, first // LIST_ROWS:(first + CHUNK) // LIST_ROWS], CHUNK, bufs=2)
            nc.scalar.activation(squashed[:, cols], picked[:], ACT.Tanh)
            apply_gain = gain_on_scalar if chunk == SCALAR_GAIN_CHUNK else gain_on_vector
            apply_gain(1, LAST, first, squashed)
            quantise_x(1, first)
            y = sbuf("y", [P, PACK, CHUNK], F32, f"page0{chunk}")
            y_bf = sbuf("y_bf", [P, CHUNK, PACK], BF16, "rounded", 2)
            for j in range(0, CHUNK, BANK_SLOTS):
                c = (first + j) // BANK_SLOTS
                last_product(c, 1)
                nc.scalar.copy(y[:, :, j:j + BANK_SLOTS], y_banks[c][:])
                nc.vector.tensor_copy(y_bf[:, j:j + BANK_SLOTS, :].rearrange("p (s e) t -> p s t e", e=2),
                                      y[:, :, j:j + BANK_SLOTS].rearrange("p t (s e) -> p s t e", e=2))
            nc.sync.dma_start(y_rows[:, :, cols], y[:])
            quantise(y_codes[:, cols], y_scales[:, cols], y_bf[:].rearrange("p j t -> p (j t)"))
            if chunk % 2 == 1:
                pair = slice(first - CHUNK, first + CHUNK)
                nc.sync.dma_start(y_words[:, pair], y_codes[:, pair].bitcast(I32))
        for quad in range(QUADS):
            queue = nc.scalar if quad % 2 else nc.sync
            queue.dma_start(out_2[0, 4 * quad:4 * quad + 4, :].bitcast(I32),
                            y_scales[QUAD * quad:QUAD * quad + 4, :].bitcast(I32))
